import numpy as np
import ml_dtypes


def mxq(x, axis, fmt="e4m3"):
    dtype, down = {"e4m3": (ml_dtypes.float8_e4m3fn, 7), "e5m2": (ml_dtypes.float8_e5m2, 14)}[fmt]
    v = np.moveaxis(np.asarray(x, np.float32).astype(ml_dtypes.bfloat16).astype(np.float64), axis, -1)
    blocks = v.reshape(v.shape[:-1] + (-1, 32))
    amax = np.abs(blocks).max(-1, keepdims=True)
    byte = np.maximum(np.where(amax > 0, np.frexp(amax)[1] - 1 + 127, 0) - down, 1)
    scale = np.exp2(byte - 127.0)
    codes = (blocks / scale).astype(np.float32).astype(dtype).astype(np.float64)
    return np.moveaxis((codes * scale).reshape(v.shape), -1, axis)


WIDE = False


def mx_kscale(k):
    if not WIDE:
        return np.ones(k)
    levels = np.array([10, -10, 5, -5, 0])
    if k % 512:
        return np.exp2(np.random.permutation(np.resize(levels, k // 32))).repeat(32)
    a = np.empty((k // 512, 16))
    for p in range(k // 512):
        a[p, :8] = np.random.permutation(np.resize(levels, 8))
        for g in range(8):
            far = levels[np.abs(levels - a[p, g]) >= 10]
            a[p, g + 8] = far[np.random.randint(len(far))]
    return np.exp2(a.ravel()).repeat(32)


def f64(x):
    return np.asarray(x).astype(np.float64)


def striped(idx):
    return np.tile(np.asarray(idx).reshape(-1, 16).T, (8, 1)).astype(np.uint16)


def unstriped(offs):
    return offs[:16].T.reshape(-1).astype(np.int64)


E2M1 = np.array([0.0, 0.5, 1.0, 1.5, 2.0, 3.0, 4.0, 6.0, -0.0, -0.5, -1.0, -1.5, -2.0, -3.0, -4.0, -6.0])


def pack_weight(w, fmt):
    k, n = w.shape
    w = f64(np.asarray(w, np.float32).astype(ml_dtypes.bfloat16)).reshape(k // 32, 32, n)
    amax = np.abs(w).max(1)
    if fmt == "e4m3":
        byte = np.frexp(amax)[1] - 1 + 127 - 7
    else:
        mant, ex = np.frexp(amax / 6.0)
        byte = np.where(mant > 0.5, ex, ex - 1) + 127
    byte = np.clip(np.where(amax > 0, byte, 1), 1, 254)
    scaled = (w * np.exp2(127.0 - byte)[:, None, :]).reshape(k, n).astype(np.float32)
    by_word = np.ascontiguousarray(scaled.reshape(k // 512, 128, 4, n).transpose(0, 1, 3, 2))
    if fmt == "e4m3":
        words = by_word.astype(ml_dtypes.float8_e4m3fn).view(np.uint8)
    else:
        c = by_word.astype(ml_dtypes.float4_e2m1fn).view(np.uint8) & 0xF
        words = (c[..., 0::2] | (c[..., 1::2] << 4)).reshape(k // 512, 128, 2 * n)
    return np.ascontiguousarray(words), np.ascontiguousarray(byte.astype(np.uint8).reshape(k // 512, 16, n))


def unpack_weight(words, scales, fmt):
    g, _, n = scales.shape
    words = np.ascontiguousarray(words).reshape(g, 128, n, -1)
    if fmt == "e4m3":
        vals = words.view(ml_dtypes.float8_e4m3fn).astype(np.float64)
    else:
        nib = np.empty((g, 128, n, 4), np.uint8)
        nib[..., 0::2] = words & 0xF
        nib[..., 1::2] = words >> 4
        vals = E2M1[nib]
    vals = vals * np.repeat(np.exp2(scales.astype(np.float64) - 127.0), 8, axis=1)[..., None]
    return vals.transpose(0, 1, 3, 2).reshape(g * 512, n)


B, N, T, D, DV, NQ = 2, 512, 2048, 512, 256, 256
PAGE = 16


def setup_inputs():
    n = np.random.standard_normal
    pages = np.random.permutation(T // PAGE)[:B * N // PAGE]
    idx = (pages[:, None] * PAGE + np.arange(PAGE)[None, :]).reshape(-1)
    s = mx_kscale(D)[:, None]
    u = np.ones(T)
    u[idx] = mx_kscale(B * N)
    r = np.random.uniform(0.5, 2.0, T)
    qp = [pack_weight(x, "e4m3") for x in n((B, D, NQ)) * s * (0.80 / np.sqrt(D))]
    k = n((D, T)) / s
    v = n((DV, T)) / (u * r)
    kp = pack_weight(k, "e4m3")
    return {
        "q_words": np.stack([x[0] for x in qp]),
        "q_scales": np.stack([x[1] for x in qp]),
        "k_words": kp[0],
        "k_scales": kp[1],
        "vT": v.astype(np.float32),
        "vs": np.tile(u * r, (128, 1)).astype(np.float32),
        "kb": np.tile(n(T), (128, 1)).astype(np.float32),
        "offs": striped(idx),
    }


def reference(q_words, q_scales, k_words, k_scales, vT, vs, kb, offs):
    idx = unstriped(offs)
    k = unpack_weight(k_words, k_scales, "e4m3")
    v = f64(vT)
    pick = lambda x: x[:, idx].reshape(x.shape[0], B, N).transpose(1, 0, 2)
    q = np.stack([unpack_weight(q_words[b], q_scales[b], "e4m3") for b in range(B)])
    score = q.transpose(0, 2, 1) @ pick(k)
    score = score + pick(f64(kb))[:, :1, :]
    p = 1.0 / (1.0 + np.exp(-score))
    w = p * pick(f64(vs))[:, :1, :]
    y = mxq(w, 2, "e4m3") @ mxq(pick(v).transpose(0, 2, 1), 1, "e4m3")
    y = y / 16.0
    return y

@@ -1,0 +1,196 @@
+from contextlib import ExitStack
+
+import concourse.mybir as mybir
+from concourse.masks import make_identity
+
+B, N, T, D, DV, NQ = 2, 512, 2048, 512, 256, 256
+FLOPS = 2 * B * NQ * N * (D + DV)
+
+F32 = mybir.dt.float32
+BF16 = mybir.dt.bfloat16
+I32 = mybir.dt.int32
+U32 = mybir.dt.uint32
+U16 = mybir.dt.uint16
+U8 = mybir.dt.uint8
+FP8X4 = mybir.dt.float8_e4m3fn_x4
+ACT = mybir.ActivationFunctionType
+ALU = mybir.AluOpType
+
+P = 128
+PACK = 4
+RUN = 8
+ROW = P - 1
+V_CHUNKS = 4
+LIST_COLS = N // 16
+
+
+def dealt(view):
+    return view.rearrange("p j (g i) -> p g j i", i=RUN)
+
+
+def tile_attend_sigm_kb_pgb2q256n512t2048_kernel(tc, q_words, q_scales, k_words, k_scales, vT, vs, kb, offs, out):
+    nc = tc.nc
+    with ExitStack() as ctx:
+        sb = ctx.enter_context(tc.tile_pool(name="sb", bufs=1))
+        ps = ctx.enter_context(tc.psum_pool(name="ps", bufs=1))
+
+        offsets = sb.tile([P, B * LIST_COLS], U16, name="offsets")
+        kb_pool = sb.tile([P, T], F32, name="kb_pool")
+        vs_pool = sb.tile([P, T], F32, name="vs_pool")
+        kw_pool = sb.tile([P, T], U32, name="kw_pool")
+        ks_pool = sb.tile([P, T], U8, name="ks_pool")
+        qw = sb.tile([P, B, NQ], U32, name="qw", align_bytes=64)
+        qs = sb.tile([P, B, NQ], U8, name="qs", align_bytes=64)
+        ident = sb.tile([P, P], F32, name="ident")
+        warm = sb.tile([P, 2], F32, name="warm")
+
+        nc.gpsimd.memset(ks_pool[:].bitcast(I32), 0)
+        nc.gpsimd.memset(qs[:].rearrange("p b q -> p (b q)").bitcast(I32), 0)
+        nc.vector.memset(warm[:, 0:1], 0.0)
+        nc.vector.memset(kb_pool[0:ROW, :], 0.0)
+        nc.vector.memset(vs_pool[0:ROW, :], 0.0)
+        make_identity(nc, ident[:])
+        nc.scalar.activation(warm[:, 1:2], warm[:, 0:1], ACT.Sigmoid)
+
+        nc.sync.dma_start(offsets[:], offs)
+        nc.sync.dma_start(kb_pool[ROW:P, :], kb[0:1, :])
+        nc.sync.dma_start(vs_pool[ROW:P, :], vs[0:1, :])
+        nc.sync.dma_start(kw_pool[:].bitcast(I32), k_words[0].rearrange("p t r -> p (t r)").bitcast(I32))
+        ks_rows = k_scales[0].bitcast(I32).rearrange("(a r) t -> r a t", r=4)
+        for r in range(4):
+            nc.sync.dma_start(ks_pool[:].bitcast(I32)[r:P:32, :], ks_rows[r])
+
+        chunk = T // V_CHUNKS
+        v_rows = vT.rearrange("(p h) t -> p h t", h=2)
+        v_pairs = sb.tile([P, T * 2], BF16, name="v_pairs")
+        v_raw = []
+        for c in range(V_CHUNKS):
+            raw = sb.tile([P, 2, chunk], F32, name="v_raw%d" % c)
+            v_raw.append(raw)
+            nc.sync.dma_start(raw[:], v_rows[:, :, c * chunk:(c + 1) * chunk])
+        nc.sync.dma_start(qw[:].bitcast(I32), q_words.rearrange("b o p q r -> p (b o) (q r)").bitcast(I32))
+        qs_rows = q_scales.bitcast(I32).rearrange("b o (a r) q -> r a (b o) q", r=4)
+        for r in range(4):
+            nc.sync.dma_start(qs[:].bitcast(I32)[r:P:32, :, :], qs_rows[r])
+        for c in range(V_CHUNKS):
+            nc.scalar.copy(
+                v_pairs[:, 2 * c * chunk:2 * (c + 1) * chunk].rearrange("p (t h) -> p t h", h=2),
+                v_raw[c][:].rearrange("p h t -> p t h"),
+            )
+
+        def slots(b):
+            return slice(b * P, (b + 1) * P)
+
+        def seq_list(b):
+            return offsets[:, b * LIST_COLS:(b + 1) * LIST_COLS]
+
+        def turn(bank, gathered, b):
+            for j in range(PACK):
+                nc.tensor.transpose(bank[:, j, :], gathered[:, j, slots(b)], ident[:])
+
+        kb_g = sb.tile([P, PACK, B * P], F32, name="kb_g")
+        nc.vector.tensor_copy(dealt(kb_g[:].bitcast(U32)), kb_pool[:].bitcast(U32).indirect(offsets[:]))
+        kb_col = sb.tile([P, B, PACK], F32, name="kb_col")
+        for b in range(B):
+            bank = ps.tile([P, PACK, P], F32, name="turn%d" % b, tag="turn%d" % b)
+            turn(bank, kb_g, b)
+            nc.scalar.copy(kb_col[:, b, :], bank[:, :, ROW])
+
+        kw_g = sb.tile([P, PACK, B * P], U32, name="kw_g", align_bytes=64)
+        nc.vector.tensor_copy(dealt(kw_g[:]), kw_pool[:].indirect(offsets[:]))
+        ks_g = sb.tile([P, B * N], U8, name="ks_g")
+        nc.vector.tensor_copy(ks_g[:], ks_pool[:].indirect(offsets[:]))
+        ks_d = sb.tile([P, PACK, B * P], U8, name="ks_d", align_bytes=64)
+        nc.vector.tensor_copy(
+            ks_d[:].bitcast(I32).rearrange("p j (g i) -> p j g i", i=RUN // 4),
+            ks_g[:].bitcast(I32).rearrange("p (g j i) -> p j g i", j=PACK, i=RUN // 4),
+        )
+
+        prob = []
+        for b in range(B):
+            p_b = sb.tile([P, PACK, NQ], F32, name="prob%d" % b)
+            prob.append(p_b)
+            for half in range(2):
+                bank = ps.tile([P, 2, NQ], F32, name="score%d%d" % (b, half), tag="score%d%d" % (b, half))
+                for u in range(2):
+                    j = 2 * half + u
+                    nc.tensor.matmul_mx(
+                        out=bank[:, u, :],
+                        lhsT=kw_g[:, j, slots(b)].bitcast(FP8X4), lhsT_scale=ks_d[:, j, slots(b)],
+                        rhs=qw[:, b, :].bitcast(FP8X4), rhs_scale=qs[:, b, :],
+                        start=True, stop=True,
+                    )
+                for u in range(2):
+                    j = 2 * half + u
+                    nc.scalar.activation(p_b[:, j, :], bank[:, u, :], ACT.Sigmoid, bias=kb_col[:, b, j:j + 1])
+
+        vs_g = sb.tile([P, PACK, B * P], F32, name="vs_g")
+        nc.vector.tensor_copy(dealt(vs_g[:].bitcast(U32)), vs_pool[:].bitcast(U32).indirect(offsets[:]))
+        vs_bank = []
+        for b in range(B):
+            bank = ps.tile([P, PACK, P], F32, name="vs_bank%d" % b, tag="vs_bank%d" % b)
+            vs_bank.append(bank)
+            turn(bank, vs_g, b)
+
+        v_bf = []
+        for b in range(B):
+            v_g = sb.tile([P, PACK, P], F32, name="v_g%d" % b)
+            nc.vector.tensor_copy(dealt(v_g[:].bitcast(U32)), v_pairs[:].bitcast(U32).indirect(seq_list(b)))
+            bank = ps.tile([P, PACK, P], F32, name="vturn%d" % b, tag="turn%d" % b)
+            turn(bank, v_g, 0)
+            v_b = sb.tile([P, DV * PACK], BF16, name="v_bf%d" % b, align_bytes=64)
+            v_bf.append(v_b)
+            nc.scalar.copy(
+                v_b[:].rearrange("p (e j) -> p e j", j=PACK),
+                bank[:].bitcast(BF16).rearrange("p j e -> p e j"),
+            )
+
+        w_bf = [sb.tile([P, NQ * PACK], BF16, name="w_bf%d" % b, align_bytes=64) for b in range(B)]
+        v_codes = [sb.tile([P, DV], U32, name="v_codes%d" % b, align_bytes=64) for b in range(B)]
+        v_sc = [sb.tile([P, DV], U8, name="v_sc%d" % b, align_bytes=64) for b in range(B)]
+        w_codes = [sb.tile([P, NQ], U32, name="w_codes%d" % b, align_bytes=64) for b in range(B)]
+        w_sc = [sb.tile([P, NQ], U8, name="w_sc%d" % b, align_bytes=64) for b in range(B)]
+
+        def weigh(b, q0, q1):
+            scale = vs_bank[b][:, :, ROW:P].unsqueeze(1).to_broadcast([P, (q1 - q0) // 4, PACK, 4])
+            nc.vector.tensor_tensor(
+                w_bf[b][:, q0 * PACK:q1 * PACK].rearrange("p (c i j) -> p c j i", i=4, j=PACK),
+                prob[b][:, :, q0:q1].rearrange("p j (c i) -> p c j i", i=4),
+                scale, ALU.mult,
+            )
+
+        def quantize_w(b, q0, q1):
+            nc.vector.quantize_mx(out=w_codes[b][:, q0:q1].bitcast(FP8X4), scales=w_sc[b][:, q0:q1],
+                                  in_=w_bf[b][:, q0 * PACK:q1 * PACK])
+
+        def quantize_v(b):
+            nc.vector.quantize_mx(out=v_codes[b][:].bitcast(FP8X4), scales=v_sc[b][:], in_=v_bf[b][:])
+
+        def finish(b, m, on_vector):
+            rows = slice(m * P, (m + 1) * P)
+            acc = ps.tile([P, 2, NQ], F32, name="acc%d%d" % (b, m), tag="score%d%d" % (b, m))
+            nc.tensor.matmul_mx(
+                out=acc[:, 0, :],
+                lhsT=w_codes[b][:, rows].bitcast(FP8X4), lhsT_scale=w_sc[b][:, rows],
+                rhs=v_codes[b][:].bitcast(FP8X4), rhs_scale=v_sc[b][:],
+                start=True, stop=True,
+            )
+            y = sb.tile([P, DV], F32, name="y%d%d" % (b, m))
+            if on_vector:
+                nc.vector.tensor_scalar(y[:], acc[:, 0, :], 1.0 / 16.0, None, ALU.mult)
+            else:
+                nc.scalar.activation(y[:], acc[:, 0, :], ACT.Copy, scale=1.0 / 16.0)
+            nc.sync.dma_start(out[b, rows, :], y[:])
+
+        weigh(0, 0, NQ)
+        quantize_v(0)
+        quantize_w(0, 0, NQ)
+        finish(0, 0, False)
+        finish(0, 1, False)
+        weigh(1, 0, P)
+        quantize_v(1)
+        weigh(1, P, NQ)
+        quantize_w(1, 0, P)
+        quantize_w(1, P, NQ)
+        finish(1, 0, False)
+        finish(1, 1, True)

@@ -18,97 +18,149 @@ ALU = mybir.AluOpType
 
 P = 128
 PACK = 4
-RUN = 8
 ROW = P - 1
-V_CHUNKS = 4
+HALVES = DV // P
+CHUNKS = 2
 LIST_COLS = N // 16
-
-
-def dealt(view):
-    return view.rearrange("p j (g i) -> p g j i", i=RUN)
 
 
 def tile_attend_sigm_kb_pgb2q256n512t2048_kernel(tc, q_words, q_scales, k_words, k_scales, vT, vs, kb, offs, out):
     nc = tc.nc
     with ExitStack() as ctx:
         sb = ctx.enter_context(tc.tile_pool(name="sb", bufs=1))
+        late = ctx.enter_context(tc.tile_pool(name="late", bufs=1))
         ps = ctx.enter_context(tc.psum_pool(name="ps", bufs=1))
 
         offsets = sb.tile([P, B * LIST_COLS], U16, name="offsets")
         kb_pool = sb.tile([P, T], F32, name="kb_pool")
-        vs_pool = sb.tile([P, T], F32, name="vs_pool")
-        kw_pool = sb.tile([P, T], U32, name="kw_pool")
+        vs_pool = sb.tile([P, T], F32, name="vs_pool", tag="vs_pool", align_bytes=64)
         ks_pool = sb.tile([P, T], U8, name="ks_pool")
-        qw = sb.tile([P, B, NQ], U32, name="qw", align_bytes=64)
-        qs = sb.tile([P, B, NQ], U8, name="qs", align_bytes=64)
         ident = sb.tile([P, P], F32, name="ident")
-        warm = sb.tile([P, 2], F32, name="warm")
+        chunk = T // CHUNKS
+        kw_at = CHUNKS * chunk * 4
+        qw_at = kw_at + T * 4
+        qs_at = qw_at + B * NQ * 4
+        late_bytes = qs_at + B * NQ
+        warm = late.tile([P, late_bytes // 4], F32, name="warm", offset=0, align_bytes=64)
 
         nc.gpsimd.memset(ks_pool[:].bitcast(I32), 0)
-        nc.gpsimd.memset(qs[:].rearrange("p b q -> p (b q)").bitcast(I32), 0)
         nc.vector.memset(warm[:, 0:1], 0.0)
         nc.vector.memset(kb_pool[0:ROW, :], 0.0)
         nc.vector.memset(vs_pool[0:ROW, :], 0.0)
         make_identity(nc, ident[:])
         nc.scalar.activation(warm[:, 1:2], warm[:, 0:1], ACT.Sigmoid)
 
+        v_raw = [
+            [sb.tile([P, chunk], F32, name="v_raw0%d" % c) for c in range(CHUNKS)],
+            [late.tile([P, chunk], F32, name="v_raw1%d" % c, offset=c * chunk * 4, align_bytes=64) for c in range(CHUNKS)],
+        ]
+        kw_pool = late.tile([P, T], U32, name="kw_pool", offset=kw_at, align_bytes=64)
+        qw = late.tile([P, B, NQ], U32, name="qw", offset=qw_at, align_bytes=64)
+        qs = late.tile([P, B, NQ], U8, name="qs", offset=qs_at, align_bytes=64)
+        nc.gpsimd.memset(qs[:].rearrange("p b q -> p (b q)").bitcast(I32), 0)
+
+        def load_values(h, c):
+            nc.sync.dma_start(v_raw[h][c][:], vT[h * P:(h + 1) * P, c * chunk:(c + 1) * chunk])
+
         nc.sync.dma_start(offsets[:], offs)
         nc.sync.dma_start(kb_pool[ROW:P, :], kb[0:1, :])
         nc.sync.dma_start(vs_pool[ROW:P, :], vs[0:1, :])
-        nc.sync.dma_start(kw_pool[:].bitcast(I32), k_words[0].rearrange("p t r -> p (t r)").bitcast(I32))
+        load_values(0, 0)
+        load_values(0, 1)
         ks_rows = k_scales[0].bitcast(I32).rearrange("(a r) t -> r a t", r=4)
         for r in range(4):
             nc.sync.dma_start(ks_pool[:].bitcast(I32)[r:P:32, :], ks_rows[r])
-
-        chunk = T // V_CHUNKS
-        v_rows = vT.rearrange("(p h) t -> p h t", h=2)
-        v_pairs = sb.tile([P, T * 2], BF16, name="v_pairs")
-        v_raw = []
-        for c in range(V_CHUNKS):
-            raw = sb.tile([P, 2, chunk], F32, name="v_raw%d" % c)
-            v_raw.append(raw)
-            nc.sync.dma_start(raw[:], v_rows[:, :, c * chunk:(c + 1) * chunk])
+        load_values(1, 0)
+        load_values(1, 1)
+        nc.sync.dma_start(kw_pool[:].bitcast(I32), k_words[0].rearrange("p t r -> p (t r)").bitcast(I32))
         nc.sync.dma_start(qw[:].bitcast(I32), q_words.rearrange("b o p q r -> p (b o) (q r)").bitcast(I32))
         qs_rows = q_scales.bitcast(I32).rearrange("b o (a r) q -> r a (b o) q", r=4)
         for r in range(4):
             nc.sync.dma_start(qs[:].bitcast(I32)[r:P:32, :, :], qs_rows[r])
-        for c in range(V_CHUNKS):
-            nc.scalar.copy(
-                v_pairs[:, 2 * c * chunk:2 * (c + 1) * chunk].rearrange("p (t h) -> p t h", h=2),
-                v_raw[c][:].rearrange("p h t -> p t h"),
-            )
-
-        def slots(b):
-            return slice(b * P, (b + 1) * P)
 
         def seq_list(b):
             return offsets[:, b * LIST_COLS:(b + 1) * LIST_COLS]
 
-        def turn(bank, gathered, b):
+        def turn_row(bank, gathered):
             for j in range(PACK):
-                nc.tensor.transpose(bank[:, j, :], gathered[:, j, slots(b)], ident[:])
+                nc.tensor.transpose(bank[:, j, :], gathered[:, j:N:PACK], ident[:])
 
-        kb_g = sb.tile([P, PACK, B * P], F32, name="kb_g")
-        nc.vector.tensor_copy(dealt(kb_g[:].bitcast(U32)), kb_pool[:].bitcast(U32).indirect(offsets[:]))
-        kb_col = sb.tile([P, B, PACK], F32, name="kb_col")
-        for b in range(B):
-            bank = ps.tile([P, PACK, P], F32, name="turn%d" % b, tag="turn%d" % b)
-            turn(bank, kb_g, b)
-            nc.scalar.copy(kb_col[:, b, :], bank[:, :, ROW])
-
-        kw_g = sb.tile([P, PACK, B * P], U32, name="kw_g", align_bytes=64)
-        nc.vector.tensor_copy(dealt(kw_g[:]), kw_pool[:].indirect(offsets[:]))
+        kb_g = sb.tile([P, B, N], F32, name="kb_g")
+        nc.vector.tensor_copy(kb_g[:].rearrange("p b n -> p (b n)"), kb_pool[:].indirect(offsets[:]))
         ks_g = sb.tile([P, B * N], U8, name="ks_g")
         nc.vector.tensor_copy(ks_g[:], ks_pool[:].indirect(offsets[:]))
+
+        vs_g = []
+        vs_bank = []
+
+        def gather_scales(b, tag):
+            vs_g.append(sb.tile([P, N], F32, name="vs_g%d" % b, tag=tag))
+            nc.vector.tensor_copy(vs_g[b][:], vs_pool[:].indirect(seq_list(b)))
+
+        def turn_scales(b, bank_tag):
+            vs_bank.append(ps.tile([P, PACK, P], F32, name="vs_bank%d" % b, tag=bank_tag))
+            turn_row(vs_bank[b], vs_g[b])
+
+        v_pool = [sb.tile([P, T], BF16, name="v_pool%d" % h) for h in range(HALVES)]
+        v_g = [sb.tile([P, HALVES, N], BF16, name="v_g%d" % b) for b in range(B)]
+
+        def cast_values(h, c):
+            nc.scalar.copy(v_pool[h][:, c * chunk:(c + 1) * chunk], v_raw[h][c][:])
+
+        def gather_values(h, b):
+            nc.scalar.activation(v_g[b][:, h, :], v_pool[h][:].indirect(seq_list(b)), ACT.Copy)
+
+        def turn_values(b, bank_tag, v_b, copy):
+            bank = ps.tile([P, 2 * HALVES, P], F32, name="v_bank%d" % b, tag=bank_tag)
+            for h in range(HALVES):
+                words = v_g[b][:, h, :].bitcast(F32)
+                for u in range(2):
+                    nc.tensor.transpose(bank[:, 2 * h + u, :], words[:, u:N // 2:2], ident[:])
+            copy(
+                v_b[:].bitcast(F32).rearrange("p (h e u) -> p h e u", h=HALVES, u=2),
+                bank[:].rearrange("p (h u) e -> p h e u", u=2),
+            )
+
+        cast_values(0, 0)
+        cast_values(0, 1)
+        gather_values(0, 0)
+        gather_values(0, 1)
+        cast_values(1, 0)
+        kb_col = late.tile([P, B, PACK], F32, name="kb_col", offset=0, align_bytes=64)
+        for b in range(B):
+            bank = ps.tile([P, PACK, P], F32, name="kb_bank%d" % b, tag="turn%d" % b)
+            turn_row(bank, kb_g[:, b, :])
+            nc.scalar.copy(kb_col[:, b, :], bank[:, :, ROW])
+        cast_values(1, 1)
+        gather_values(1, 0)
+        gather_values(1, 1)
+
+        gather_scales(0, "vs_g0")
+        turn_scales(0, "vs_bank0")
         ks_d = sb.tile([P, PACK, B * P], U8, name="ks_d", align_bytes=64)
         nc.vector.tensor_copy(
-            ks_d[:].bitcast(I32).rearrange("p j (g i) -> p j g i", i=RUN // 4),
-            ks_g[:].bitcast(I32).rearrange("p (g j i) -> p j g i", j=PACK, i=RUN // 4),
+            ks_d[:].rearrange("p j (c i) -> p c j i", i=16),
+            ks_g[:].rearrange("p (c i j) -> p c j i", i=16, j=PACK),
         )
+        kw_g = [sb.tile([P, N], U32, name="kw_g%d" % b, tag="kw_g%d" % b) for b in range(B)]
+        kw_d = [sb.tile([P, PACK, P], U32, name="kw_d%d" % b, align_bytes=64) for b in range(B)]
+        for b in range(B):
+            nc.vector.tensor_copy(kw_g[b][:], kw_pool[:].indirect(seq_list(b)))
+        for b in range(B):
+            nc.vector.tensor_copy(
+                kw_d[b][:].bitcast(I32).rearrange("p j (c i) -> p c j i", i=4),
+                kw_g[b][:].bitcast(I32).rearrange("p (c i j) -> p c j i", i=4, j=PACK),
+            )
+        gather_scales(1, "kw_g1")
+        v_bf = [
+            sb.tile([P, DV * PACK], BF16, name="v_bf0", align_bytes=64, tag="vs_pool"),
+            late.tile([P, DV * PACK], BF16, name="v_bf1", align_bytes=64, offset=0),
+        ]
+        turn_values(0, "turn0", v_bf[0], nc.vector.tensor_copy)
 
         prob = []
         for b in range(B):
-            p_b = sb.tile([P, PACK, NQ], F32, name="prob%d" % b)
+            p_b = sb.tile([P, PACK, NQ], F32, name="prob%d" % b, align_bytes=64, tag="prob%d" % b)
             prob.append(p_b)
             for half in range(2):
                 bank = ps.tile([P, 2, NQ], F32, name="score%d%d" % (b, half), tag="score%d%d" % (b, half))
@@ -116,40 +168,22 @@ def tile_attend_sigm_kb_pgb2q256n512t2048_kernel(tc, q_words, q_scales, k_words,
                     j = 2 * half + u
                     nc.tensor.matmul_mx(
                         out=bank[:, u, :],
-                        lhsT=kw_g[:, j, slots(b)].bitcast(FP8X4), lhsT_scale=ks_d[:, j, slots(b)],
+                        lhsT=kw_d[b][:, j, :].bitcast(FP8X4), lhsT_scale=ks_d[:, j, b * P:(b + 1) * P],
                         rhs=qw[:, b, :].bitcast(FP8X4), rhs_scale=qs[:, b, :],
                         start=True, stop=True,
                     )
                 for u in range(2):
                     j = 2 * half + u
                     nc.scalar.activation(p_b[:, j, :], bank[:, u, :], ACT.Sigmoid, bias=kb_col[:, b, j:j + 1])
-
-        vs_g = sb.tile([P, PACK, B * P], F32, name="vs_g")
-        nc.vector.tensor_copy(dealt(vs_g[:].bitcast(U32)), vs_pool[:].bitcast(U32).indirect(offsets[:]))
-        vs_bank = []
-        for b in range(B):
-            bank = ps.tile([P, PACK, P], F32, name="vs_bank%d" % b, tag="vs_bank%d" % b)
-            vs_bank.append(bank)
-            turn(bank, vs_g, b)
-
-        v_bf = []
-        for b in range(B):
-            v_g = sb.tile([P, PACK, P], F32, name="v_g%d" % b)
-            nc.vector.tensor_copy(dealt(v_g[:].bitcast(U32)), v_pairs[:].bitcast(U32).indirect(seq_list(b)))
-            bank = ps.tile([P, PACK, P], F32, name="vturn%d" % b, tag="turn%d" % b)
-            turn(bank, v_g, 0)
-            v_b = sb.tile([P, DV * PACK], BF16, name="v_bf%d" % b, align_bytes=64)
-            v_bf.append(v_b)
-            nc.scalar.copy(
-                v_b[:].rearrange("p (e j) -> p e j", j=PACK),
-                bank[:].bitcast(BF16).rearrange("p j e -> p e j"),
-            )
+        turn_values(1, "score00", v_bf[1], nc.scalar.copy)
+        turn_scales(1, "score01")
 
         w_bf = [sb.tile([P, NQ * PACK], BF16, name="w_bf%d" % b, align_bytes=64) for b in range(B)]
-        v_codes = [sb.tile([P, DV], U32, name="v_codes%d" % b, align_bytes=64) for b in range(B)]
+        v_codes = [sb.tile([P, DV], U32, name="v_codes%d" % b, align_bytes=64, tag=("prob0", "v_codes1")[b]) for b in range(B)]
         v_sc = [sb.tile([P, DV], U8, name="v_sc%d" % b, align_bytes=64) for b in range(B)]
-        w_codes = [sb.tile([P, NQ], U32, name="w_codes%d" % b, align_bytes=64) for b in range(B)]
+        w_codes = [sb.tile([P, NQ], U32, name="w_codes%d" % b, align_bytes=64, tag=("vs_pool", "w_codes1")[b]) for b in range(B)]
         w_sc = [sb.tile([P, NQ], U8, name="w_sc%d" % b, align_bytes=64) for b in range(B)]
+        acc_tags = (("turn1", "acc01"), ("score10", "score11"))
 
         def weigh(b, q0, q1):
             scale = vs_bank[b][:, :, ROW:P].unsqueeze(1).to_broadcast([P, (q1 - q0) // 4, PACK, 4])
@@ -168,7 +202,7 @@ def tile_attend_sigm_kb_pgb2q256n512t2048_kernel(tc, q_words, q_scales, k_words,
 
         def finish(b, m, on_vector):
             rows = slice(m * P, (m + 1) * P)
-            acc = ps.tile([P, 2, NQ], F32, name="acc%d%d" % (b, m), tag="score%d%d" % (b, m))
+            acc = ps.tile([P, 2, NQ], F32, name="acc%d%d" % (b, m), tag=acc_tags[b][m])
             nc.tensor.matmul_mx(
                 out=acc[:, 0, :],
                 lhsT=w_codes[b][:, rows].bitcast(FP8X4), lhsT_scale=w_sc[b][:, rows],
@@ -188,8 +222,8 @@ def tile_attend_sigm_kb_pgb2q256n512t2048_kernel(tc, q_words, q_scales, k_words,
         finish(0, 0, False)
         finish(0, 1, False)
         weigh(1, 0, P)
-        quantize_v(1)
         weigh(1, P, NQ)
+        quantize_v(1)
         quantize_w(1, 0, P)
         quantize_w(1, P, NQ)
         finish(1, 0, False)

@@ -46,8 +46,8 @@ def tile_attend_sigm_kb_pgb2q256n512t2048_kernel(tc, q_words, q_scales, k_words,
         nc.gpsimd.memset(ks_pool[:].bitcast(I32), 0)
         nc.vector.memset(warm[:, 0:1], 0.0)
         nc.vector.memset(kb_pool[0:ROW, :], 0.0)
-        nc.vector.memset(vs_pool[0:ROW, :], 0.0)
         make_identity(nc, ident[:])
+        nc.gpsimd.memset(vs_pool[0:ROW, :], 0.0)
         nc.scalar.activation(warm[:, 1:2], warm[:, 0:1], ACT.Sigmoid)
 
         v_raw = [
@@ -57,7 +57,7 @@ def tile_attend_sigm_kb_pgb2q256n512t2048_kernel(tc, q_words, q_scales, k_words,
         kw_pool = late.tile([P, T], U32, name="kw_pool", offset=kw_at, align_bytes=64)
         qw = late.tile([P, B, NQ], U32, name="qw", offset=qw_at, align_bytes=64)
         qs = late.tile([P, B, NQ], U8, name="qs", offset=qs_at, align_bytes=64)
-        nc.gpsimd.memset(qs[:].rearrange("p b q -> p (b q)").bitcast(I32), 0)
+        nc.vector.memset(qs[:].rearrange("p b q -> p (b q)").bitcast(I32), 0)
 
         def load_values(h, c):
             nc.sync.dma_start(v_raw[h][c][:], vT[h * P:(h + 1) * P, c * chunk:(c + 1) * chunk])

@@ -18,213 +18,199 @@ ALU = mybir.AluOpType
 
 P = 128
 PACK = 4
+RUN = 8
 ROW = P - 1
 HALVES = DV // P
-CHUNKS = 2
+CHUNK = T // 2
+CHUNK_BYTES = CHUNK * 4
 LIST_COLS = N // 16
+TURN_STEP = 8
 
 
 def tile_attend_sigm_kb_pgb2q256n512t2048_kernel(tc, q_words, q_scales, k_words, k_scales, vT, vs, kb, offs, out):
     nc = tc.nc
     with ExitStack() as ctx:
         sb = ctx.enter_context(tc.tile_pool(name="sb", bufs=1))
-        late = ctx.enter_context(tc.tile_pool(name="late", bufs=1))
+        shared = ctx.enter_context(tc.tile_pool(name="shared", bufs=1))
         ps = ctx.enter_context(tc.psum_pool(name="ps", bufs=1))
 
         offsets = sb.tile([P, B * LIST_COLS], U16, name="offsets")
         kb_pool = sb.tile([P, T], F32, name="kb_pool")
-        vs_pool = sb.tile([P, T], F32, name="vs_pool", tag="vs_pool", align_bytes=64)
+        vs_pool = sb.tile([P, T], F32, name="vs_pool")
         ks_pool = sb.tile([P, T], U8, name="ks_pool")
+        kw_pool = sb.tile([P, T], U32, name="kw_pool")
         ident = sb.tile([P, P], F32, name="ident")
-        chunk = T // CHUNKS
-        kw_at = CHUNKS * chunk * 4
-        qw_at = kw_at + T * 4
-        qs_at = qw_at + B * NQ * 4
-        late_bytes = qs_at + B * NQ
-        warm = late.tile([P, late_bytes // 4], F32, name="warm", offset=0, align_bytes=64)
 
         nc.gpsimd.memset(ks_pool[:].bitcast(I32), 0)
+        warm = sb.tile([P, 2], F32, name="warm")
         nc.vector.memset(warm[:, 0:1], 0.0)
         nc.vector.memset(kb_pool[0:ROW, :], 0.0)
         make_identity(nc, ident[:])
-        nc.gpsimd.memset(vs_pool[0:ROW, :], 0.0)
         nc.scalar.activation(warm[:, 1:2], warm[:, 0:1], ACT.Sigmoid)
 
-        v_raw = [
-            [sb.tile([P, chunk], F32, name="v_raw0%d" % c) for c in range(CHUNKS)],
-            [late.tile([P, chunk], F32, name="v_raw1%d" % c, offset=c * chunk * 4, align_bytes=64) for c in range(CHUNKS)],
-        ]
-        kw_pool = late.tile([P, T], U32, name="kw_pool", offset=kw_at, align_bytes=64)
-        qw = late.tile([P, B, NQ], U32, name="qw", offset=qw_at, align_bytes=64)
-        qs = late.tile([P, B, NQ], U8, name="qs", offset=qs_at, align_bytes=64)
-        nc.vector.memset(qs[:].rearrange("p b q -> p (b q)").bitcast(I32), 0)
+        def raw_values(name, at):
+            return shared.tile([P, CHUNK], F32, name=name, offset=at, align_bytes=64)
+
+        v00_at, v10_at, v01_at = 0, CHUNK_BYTES - 64, 2 * CHUNK_BYTES
+        v_raw = {(0, 0): raw_values("v_raw00", v00_at), (0, 1): raw_values("v_raw01", v01_at)}
 
         def load_values(h, c):
-            nc.sync.dma_start(v_raw[h][c][:], vT[h * P:(h + 1) * P, c * chunk:(c + 1) * chunk])
+            nc.sync.dma_start(v_raw[h, c][:], vT[h * P:(h + 1) * P, c * CHUNK:(c + 1) * CHUNK])
 
         nc.sync.dma_start(offsets[:], offs)
         nc.sync.dma_start(kb_pool[ROW:P, :], kb[0:1, :])
         nc.sync.dma_start(vs_pool[ROW:P, :], vs[0:1, :])
         load_values(0, 0)
         load_values(0, 1)
+        nc.sync.dma_start(kw_pool[:].bitcast(I32), k_words[0].rearrange("p t r -> p (t r)").bitcast(I32))
         ks_rows = k_scales[0].bitcast(I32).rearrange("(a r) t -> r a t", r=4)
         for r in range(4):
-            nc.sync.dma_start(ks_pool[:].bitcast(I32)[r:P:32, :], ks_rows[r])
-        load_values(1, 0)
-        load_values(1, 1)
-        nc.sync.dma_start(kw_pool[:].bitcast(I32), k_words[0].rearrange("p t r -> p (t r)").bitcast(I32))
-        nc.sync.dma_start(qw[:].bitcast(I32), q_words.rearrange("b o p q r -> p (b o) (q r)").bitcast(I32))
-        qs_rows = q_scales.bitcast(I32).rearrange("b o (a r) q -> r a (b o) q", r=4)
-        for r in range(4):
-            nc.sync.dma_start(qs[:].bitcast(I32)[r:P:32, :, :], qs_rows[r])
+            nc.scalar.dma_start(ks_pool[:].bitcast(I32)[r:P:32, :], ks_rows[r])
+        nc.gpsimd.memset(vs_pool[0:ROW, :], 0.0)
 
         def seq_list(b):
             return offsets[:, b * LIST_COLS:(b + 1) * LIST_COLS]
 
-        def turn_row(bank, gathered):
-            for j in range(PACK):
-                nc.tensor.transpose(bank[:, j, :], gathered[:, j:N:PACK], ident[:])
+        def dealt(ap):
+            return ap.rearrange("p t (g i) -> p g t i", i=RUN)
 
-        kb_g = sb.tile([P, B, N], F32, name="kb_g")
-        nc.vector.tensor_copy(kb_g[:].rearrange("p b n -> p (b n)"), kb_pool[:].indirect(offsets[:]))
-        ks_g = sb.tile([P, B * N], U8, name="ks_g")
+        def turn_rows(bank, rows):
+            last = len(rows) - 1
+            cols = []
+            for n, row in enumerate(rows):
+                at = (last - n) * TURN_STEP
+                nc.tensor.transpose(bank[:, at:at + P], row, ident[:])
+                cols.append(at + ROW)
+            return cols
+
+        kb_g = sb.tile([P, PACK, B * P], F32, name="kb_g")
+        nc.vector.tensor_copy(dealt(kb_g[:].bitcast(U32)), kb_pool[:].bitcast(U32).indirect(offsets[:]))
+        kb_bank = ps.tile([P, N], F32, name="kb_bank", tag="bank0")
+        turn_rows(kb_bank, [kb_g[:, t, b * P:(b + 1) * P] for b in reversed(range(B)) for t in reversed(range(PACK))])
+        ks_g = sb.tile([P, B * N], U8, name="ks_g", tag="ks_g")
         nc.vector.tensor_copy(ks_g[:], ks_pool[:].indirect(offsets[:]))
-
-        vs_g = []
-        vs_bank = []
-
-        def gather_scales(b, tag):
-            vs_g.append(sb.tile([P, N], F32, name="vs_g%d" % b, tag=tag))
-            nc.vector.tensor_copy(vs_g[b][:], vs_pool[:].indirect(seq_list(b)))
-
-        def turn_scales(b, bank_tag):
-            vs_bank.append(ps.tile([P, PACK, P], F32, name="vs_bank%d" % b, tag=bank_tag))
-            turn_row(vs_bank[b], vs_g[b])
+        ks_d = sb.tile([P, PACK, B * P], U8, name="ks_d", align_bytes=64)
+        nc.vector.tensor_copy(
+            ks_d[:].bitcast(I32).rearrange("p t (g w) -> p g t w", w=2),
+            ks_g[:].bitcast(I32).rearrange("p (g t w) -> p g t w", t=PACK, w=2),
+        )
+        kb_col = sb.tile([P, B * PACK], F32, name="kb_col", tag="ks_g")
+        nc.vector.tensor_copy(kb_col[:], kb_bank[:, ROW:ROW + B * PACK * TURN_STEP:TURN_STEP])
+        kw_d = [sb.tile([P, PACK, P], U32, name="kw_d%d" % b, align_bytes=64) for b in range(B)]
+        for b in range(B):
+            nc.vector.tensor_copy(dealt(kw_d[b][:]), kw_pool[:].indirect(seq_list(b)))
 
         v_pool = [sb.tile([P, T], BF16, name="v_pool%d" % h) for h in range(HALVES)]
         v_g = [sb.tile([P, HALVES, N], BF16, name="v_g%d" % b) for b in range(B)]
 
-        def cast_values(h, c):
-            nc.scalar.copy(v_pool[h][:, c * chunk:(c + 1) * chunk], v_raw[h][c][:])
+        def cast_values(h, c, copy):
+            copy(v_pool[h][:, c * CHUNK:(c + 1) * CHUNK], v_raw[h, c][:])
 
         def gather_values(h, b):
-            nc.scalar.activation(v_g[b][:, h, :], v_pool[h][:].indirect(seq_list(b)), ACT.Copy)
-
-        def turn_values(b, bank_tag, v_b, copy):
-            bank = ps.tile([P, 2 * HALVES, P], F32, name="v_bank%d" % b, tag=bank_tag)
-            for h in range(HALVES):
-                words = v_g[b][:, h, :].bitcast(F32)
-                for u in range(2):
-                    nc.tensor.transpose(bank[:, 2 * h + u, :], words[:, u:N // 2:2], ident[:])
-            copy(
-                v_b[:].bitcast(F32).rearrange("p (h e u) -> p h e u", h=HALVES, u=2),
-                bank[:].rearrange("p (h u) e -> p h e u", u=2),
+            nc.scalar.activation(
+                v_g[b][:, h, :].rearrange("p (g i t) -> p g t i", i=RUN, t=PACK),
+                v_pool[h][:].indirect(seq_list(b)), ACT.Copy,
             )
 
-        cast_values(0, 0)
-        cast_values(0, 1)
+        cast_values(0, 0, nc.scalar.copy)
+        cast_values(0, 1, nc.scalar.copy)
+        qw = shared.tile([P, B, NQ], U32, name="qw", offset=v00_at, align_bytes=64)
+        nc.sync.dma_start(qw[:].bitcast(I32), q_words.rearrange("b o p q r -> p (b o) (q r)").bitcast(I32))
+        v_raw[1, 0] = raw_values("v_raw10", v10_at)
+        v_raw[1, 1] = raw_values("v_raw11", v01_at)
+        load_values(1, 0)
+        qs = shared.tile([P, B, NQ], U8, name="qs", offset=v00_at + B * NQ * 4, align_bytes=64)
+        nc.gpsimd.memset(qs[:].rearrange("p b q -> p (b q)").bitcast(I32), 0)
+        qs_rows = q_scales.bitcast(I32).rearrange("b o (a r) q -> r a (b o) q", r=4)
+        for r in range(4):
+            nc.sync.dma_start(qs[:].bitcast(I32)[r:P:32, :, :], qs_rows[r])
+        load_values(1, 1)
         gather_values(0, 0)
         gather_values(0, 1)
-        cast_values(1, 0)
-        kb_col = late.tile([P, B, PACK], F32, name="kb_col", offset=0, align_bytes=64)
-        for b in range(B):
-            bank = ps.tile([P, PACK, P], F32, name="kb_bank%d" % b, tag="turn%d" % b)
-            turn_row(bank, kb_g[:, b, :])
-            nc.scalar.copy(kb_col[:, b, :], bank[:, :, ROW])
-        cast_values(1, 1)
-        gather_values(1, 0)
-        gather_values(1, 1)
+        cast_values(1, 0, nc.scalar.copy)
+        cast_values(1, 1, nc.vector.tensor_copy)
 
-        gather_scales(0, "vs_g0")
-        turn_scales(0, "vs_bank0")
-        ks_d = sb.tile([P, PACK, B * P], U8, name="ks_d", align_bytes=64)
-        nc.vector.tensor_copy(
-            ks_d[:].rearrange("p j (c i) -> p c j i", i=16),
-            ks_g[:].rearrange("p (c i j) -> p c j i", i=16, j=PACK),
-        )
-        kw_g = [sb.tile([P, N], U32, name="kw_g%d" % b, tag="kw_g%d" % b) for b in range(B)]
-        kw_d = [sb.tile([P, PACK, P], U32, name="kw_d%d" % b, align_bytes=64) for b in range(B)]
+        half_bytes = CHUNK_BYTES // 2
+        vs_g = [shared.tile([P, PACK, P], F32, name="vs_g%d" % b, offset=v01_at + b * half_bytes, align_bytes=64) for b in range(B)]
         for b in range(B):
-            nc.vector.tensor_copy(kw_g[b][:], kw_pool[:].indirect(seq_list(b)))
-        for b in range(B):
-            nc.vector.tensor_copy(
-                kw_d[b][:].bitcast(I32).rearrange("p j (c i) -> p c j i", i=4),
-                kw_g[b][:].bitcast(I32).rearrange("p (c i j) -> p c j i", i=4, j=PACK),
-            )
-        gather_scales(1, "kw_g1")
-        v_bf = [
-            sb.tile([P, DV * PACK], BF16, name="v_bf0", align_bytes=64, tag="vs_pool"),
-            late.tile([P, DV * PACK], BF16, name="v_bf1", align_bytes=64, offset=0),
+            nc.vector.tensor_copy(dealt(vs_g[b][:].bitcast(U32)), vs_pool[:].bitcast(U32).indirect(seq_list(b)))
+
+        prob = [
+            shared.tile([P, PACK, NQ], F32, name="prob0", offset=v10_at, align_bytes=64),
+            sb.tile([P, PACK, NQ], F32, name="prob1", align_bytes=64),
         ]
-        turn_values(0, "turn0", v_bf[0], nc.vector.tensor_copy)
-
-        prob = []
         for b in range(B):
-            p_b = sb.tile([P, PACK, NQ], F32, name="prob%d" % b, align_bytes=64, tag="prob%d" % b)
-            prob.append(p_b)
             for half in range(2):
-                bank = ps.tile([P, 2, NQ], F32, name="score%d%d" % (b, half), tag="score%d%d" % (b, half))
+                bank = ps.tile([P, 2, NQ], F32, name="score%d%d" % (b, half), tag="bank%d" % (1 + 2 * b + half))
                 for u in range(2):
-                    j = 2 * half + u
+                    t = 2 * half + u
                     nc.tensor.matmul_mx(
                         out=bank[:, u, :],
-                        lhsT=kw_d[b][:, j, :].bitcast(FP8X4), lhsT_scale=ks_d[:, j, b * P:(b + 1) * P],
+                        lhsT=kw_d[b][:, t, :].bitcast(FP8X4), lhsT_scale=ks_d[:, t, b * P:(b + 1) * P],
                         rhs=qw[:, b, :].bitcast(FP8X4), rhs_scale=qs[:, b, :],
                         start=True, stop=True,
                     )
                 for u in range(2):
-                    j = 2 * half + u
-                    nc.scalar.activation(p_b[:, j, :], bank[:, u, :], ACT.Sigmoid, bias=kb_col[:, b, j:j + 1])
-        turn_values(1, "score00", v_bf[1], nc.scalar.copy)
-        turn_scales(1, "score01")
+                    t = 2 * half + u
+                    c = b * PACK + t
+                    nc.scalar.activation(prob[b][:, t, :], bank[:, u, :], ACT.Sigmoid, bias=kb_col[:, c:c + 1])
+
+        vs_bank = []
+        for b in range(B):
+            vs_bank.append(ps.tile([P, N], F32, name="vs_bank%d" % b, tag="bank%d" % (1 + b)))
+            turn_rows(vs_bank[b], [vs_g[b][:, t, :] for t in reversed(range(PACK))])
+
+        gather_values(1, 0)
+        gather_values(1, 1)
+        v_bf = [sb.tile([P, DV * PACK], BF16, name="v_bf%d" % b, align_bytes=64) for b in range(B)]
+        for b in range(B):
+            bank = ps.tile([P, 2 * HALVES, P], F32, name="v_bank%d" % b, tag="bank%d" % (3 + b))
+            for h in range(HALVES):
+                words = v_g[b][:, h, :].bitcast(F32)
+                for u in range(2):
+                    nc.tensor.transpose(bank[:, 2 * h + u, :], words[:, u:N // 2:2], ident[:])
+            nc.scalar.copy(
+                v_bf[b][:].bitcast(F32).rearrange("p (h e u) -> p h e u", h=HALVES, u=2),
+                bank[:].rearrange("p (h u) e -> p h e u", u=2),
+            )
 
         w_bf = [sb.tile([P, NQ * PACK], BF16, name="w_bf%d" % b, align_bytes=64) for b in range(B)]
-        v_codes = [sb.tile([P, DV], U32, name="v_codes%d" % b, align_bytes=64, tag=("prob0", "v_codes1")[b]) for b in range(B)]
+        v_codes = [sb.tile([P, DV], U32, name="v_codes%d" % b, align_bytes=64) for b in range(B)]
         v_sc = [sb.tile([P, DV], U8, name="v_sc%d" % b, align_bytes=64) for b in range(B)]
-        w_codes = [sb.tile([P, NQ], U32, name="w_codes%d" % b, align_bytes=64, tag=("vs_pool", "w_codes1")[b]) for b in range(B)]
+        w_codes = [sb.tile([P, NQ], U32, name="w_codes%d" % b, align_bytes=64) for b in range(B)]
         w_sc = [sb.tile([P, NQ], U8, name="w_sc%d" % b, align_bytes=64) for b in range(B)]
-        acc_tags = (("turn1", "acc01"), ("score10", "score11"))
 
-        def weigh(b, q0, q1):
-            scale = vs_bank[b][:, :, ROW:P].unsqueeze(1).to_broadcast([P, (q1 - q0) // 4, PACK, 4])
+        def weigh(b):
+            scale = vs_bank[b][:, ROW:ROW + PACK * TURN_STEP:TURN_STEP].unsqueeze(1).unsqueeze(3).to_broadcast([P, NQ // 4, PACK, 4])
             nc.vector.tensor_tensor(
-                w_bf[b][:, q0 * PACK:q1 * PACK].rearrange("p (c i j) -> p c j i", i=4, j=PACK),
-                prob[b][:, :, q0:q1].rearrange("p j (c i) -> p c j i", i=4),
+                w_bf[b][:].rearrange("p (c i t) -> p c t i", i=4, t=PACK),
+                prob[b][:].rearrange("p t (c i) -> p c t i", i=4),
                 scale, ALU.mult,
             )
 
-        def quantize_w(b, q0, q1):
-            nc.vector.quantize_mx(out=w_codes[b][:, q0:q1].bitcast(FP8X4), scales=w_sc[b][:, q0:q1],
-                                  in_=w_bf[b][:, q0 * PACK:q1 * PACK])
+        def quantize(codes, scales, values):
+            nc.vector.quantize_mx(out=codes[:].bitcast(FP8X4), scales=scales[:], in_=values[:])
 
-        def quantize_v(b):
-            nc.vector.quantize_mx(out=v_codes[b][:].bitcast(FP8X4), scales=v_sc[b][:], in_=v_bf[b][:])
-
-        def finish(b, m, on_vector):
+        def finish(b, m):
             rows = slice(m * P, (m + 1) * P)
-            acc = ps.tile([P, 2, NQ], F32, name="acc%d%d" % (b, m), tag=acc_tags[b][m])
+            acc = ps.tile([P, N], F32, name="acc%d%d" % (b, m), tag="bank%d" % (0, 5, 6, 7)[2 * b + m])
             nc.tensor.matmul_mx(
-                out=acc[:, 0, :],
+                out=acc[:, 0:DV],
                 lhsT=w_codes[b][:, rows].bitcast(FP8X4), lhsT_scale=w_sc[b][:, rows],
                 rhs=v_codes[b][:].bitcast(FP8X4), rhs_scale=v_sc[b][:],
                 start=True, stop=True,
             )
             y = sb.tile([P, DV], F32, name="y%d%d" % (b, m))
-            if on_vector:
-                nc.vector.tensor_scalar(y[:], acc[:, 0, :], 1.0 / 16.0, None, ALU.mult)
+            if (b, m) == (1, 1):
+                nc.vector.tensor_scalar(y[:], acc[:, 0:DV], 1.0 / 16.0, None, ALU.mult)
             else:
-                nc.scalar.activation(y[:], acc[:, 0, :], ACT.Copy, scale=1.0 / 16.0)
+                nc.scalar.activation(y[:], acc[:, 0:DV], ACT.Copy, scale=1.0 / 16.0)
             nc.sync.dma_start(out[b, rows, :], y[:])
 
-        weigh(0, 0, NQ)
-        quantize_v(0)
-        quantize_w(0, 0, NQ)
-        finish(0, 0, False)
-        finish(0, 1, False)
-        weigh(1, 0, P)
-        weigh(1, P, NQ)
-        quantize_v(1)
-        quantize_w(1, 0, P)
-        quantize_w(1, P, NQ)
-        finish(1, 0, False)
-        finish(1, 1, True)
+        weigh(0)
+        weigh(1)
+        for b in range(B):
+            quantize(w_codes[b], w_sc[b], w_bf[b])
+            quantize(v_codes[b], v_sc[b], v_bf[b])
+            finish(b, 0)
+            finish(b, 1)

@@ -22,7 +22,8 @@ RUN = 8
 ROW = P - 1
 HALVES = DV // P
 CHUNK = T // 2
-CHUNK_BYTES = CHUNK * 4
+FIRST = 512
+LAP = 64
 LIST_COLS = N // 16
 TURN_STEP = 8
 
@@ -36,37 +37,65 @@ def tile_attend_sigm_kb_pgb2q256n512t2048_kernel(tc, q_words, q_scales, k_words,
 
         offsets = sb.tile([P, B * LIST_COLS], U16, name="offsets")
         kb_pool = sb.tile([P, T], F32, name="kb_pool")
-        vs_pool = sb.tile([P, T], F32, name="vs_pool")
         ks_pool = sb.tile([P, T], U8, name="ks_pool")
-        kw_pool = sb.tile([P, T], U32, name="kw_pool")
         ident = sb.tile([P, P], F32, name="ident")
 
-        nc.gpsimd.memset(ks_pool[:].bitcast(I32), 0)
         warm = sb.tile([P, 2], F32, name="warm")
         nc.vector.memset(warm[:, 0:1], 0.0)
+        nc.vector.memset(ks_pool[:].bitcast(I32), 0)
         nc.vector.memset(kb_pool[0:ROW, :], 0.0)
         make_identity(nc, ident[:])
         nc.scalar.activation(warm[:, 1:2], warm[:, 0:1], ACT.Sigmoid)
 
-        def raw_values(name, at):
-            return shared.tile([P, CHUNK], F32, name=name, offset=at, align_bytes=64)
+        def placed(shape, dtype, name, at):
+            return shared.tile(shape, dtype, name=name, tag="at%d" % at, offset=at, align_bytes=64)
 
-        v00_at, v10_at, v01_at = 0, CHUNK_BYTES - 64, 2 * CHUNK_BYTES
-        v_raw = {(0, 0): raw_values("v_raw00", v00_at), (0, 1): raw_values("v_raw01", v01_at)}
+        cols = {(0, 0): (0, FIRST), (0, 1): (FIRST, T), (1, 0): (0, CHUNK), (1, 1): (CHUNK, T)}
+        kw_at = 0
+        v00_at = kw_at + T * 4 - LAP
+        qs_at = v00_at + LAP
+        v10_at = v00_at + FIRST * 4 - LAP
+        v01_at = v10_at + CHUNK * 4
+        qw_at = v01_at
+        v11_at = v01_at + (T - FIRST) * 4 - LAP
+        v_at = {(0, 0): v00_at, (0, 1): v01_at, (1, 0): v10_at, (1, 1): v11_at}
+        v_raw = {}
 
         def load_values(h, c):
-            nc.sync.dma_start(v_raw[h, c][:], vT[h * P:(h + 1) * P, c * CHUNK:(c + 1) * CHUNK])
+            lo, hi = cols[h, c]
+            v_raw[h, c] = placed([P, hi - lo], F32, "v_raw%d%d" % (h, c), v_at[h, c])
+            nc.sync.dma_start(v_raw[h, c][:], vT[h * P:(h + 1) * P, lo:hi])
 
         nc.sync.dma_start(offsets[:], offs)
         nc.sync.dma_start(kb_pool[ROW:P, :], kb[0:1, :])
-        nc.sync.dma_start(vs_pool[ROW:P, :], vs[0:1, :])
         load_values(0, 0)
         load_values(0, 1)
-        nc.sync.dma_start(kw_pool[:].bitcast(I32), k_words[0].rearrange("p t r -> p (t r)").bitcast(I32))
+        vs_pool = sb.tile([P, T], F32, name="vs_pool")
+        nc.sync.dma_start(vs_pool[ROW:P, :], vs[0:1, :])
+        nc.gpsimd.memset(vs_pool[0:ROW, :], 0.0)
         ks_rows = k_scales[0].bitcast(I32).rearrange("(a r) t -> r a t", r=4)
         for r in range(4):
-            nc.scalar.dma_start(ks_pool[:].bitcast(I32)[r:P:32, :], ks_rows[r])
-        nc.gpsimd.memset(vs_pool[0:ROW, :], 0.0)
+            nc.sync.dma_start(ks_pool[:].bitcast(I32)[r:P:32, :], ks_rows[r])
+
+        v_pool = [sb.tile([P, T], BF16, name="v_pool%d" % h) for h in range(HALVES)]
+
+        def cast_values(h, c, copy):
+            lo, hi = cols[h, c]
+            copy(v_pool[h][:, lo:hi], v_raw[h, c][:])
+
+        cast_values(0, 0, nc.scalar.copy)
+        kw_pool = placed([P, T], U32, "kw_pool", kw_at)
+        nc.sync.dma_start(kw_pool[:].bitcast(I32), k_words[0].rearrange("p t r -> p (t r)").bitcast(I32))
+        load_values(1, 0)
+        qs = placed([P, B, NQ], U8, "qs", qs_at)
+        nc.gpsimd.memset(qs[:].rearrange("p b q -> p (b q)").bitcast(I32), 0)
+        qs_rows = q_scales.bitcast(I32).rearrange("b o (a r) q -> r a (b o) q", r=4)
+        for r in range(4):
+            nc.sync.dma_start(qs[:].bitcast(I32)[r:P:32, :, :], qs_rows[r])
+        cast_values(0, 1, nc.scalar.copy)
+        qw = placed([P, B, NQ], U32, "qw", qw_at)
+        nc.sync.dma_start(qw[:].bitcast(I32), q_words.rearrange("b o p q r -> p (b o) (q r)").bitcast(I32))
+        load_values(1, 1)
 
         def seq_list(b):
             return offsets[:, b * LIST_COLS:(b + 1) * LIST_COLS]
@@ -96,47 +125,33 @@ def tile_attend_sigm_kb_pgb2q256n512t2048_kernel(tc, q_words, q_scales, k_words,
         )
         kb_col = sb.tile([P, B * PACK], F32, name="kb_col", tag="ks_g")
         nc.vector.tensor_copy(kb_col[:], kb_bank[:, ROW:ROW + B * PACK * TURN_STEP:TURN_STEP])
-        kw_d = [sb.tile([P, PACK, P], U32, name="kw_d%d" % b, align_bytes=64) for b in range(B)]
+        kw_d = [sb.tile([P, PACK, P], U32, name="kw_d%d" % b, tag="kw_d%d" % b, align_bytes=64) for b in range(B)]
         for b in range(B):
             nc.vector.tensor_copy(dealt(kw_d[b][:]), kw_pool[:].indirect(seq_list(b)))
 
-        v_pool = [sb.tile([P, T], BF16, name="v_pool%d" % h) for h in range(HALVES)]
-        v_g = [sb.tile([P, HALVES, N], BF16, name="v_g%d" % b) for b in range(B)]
-
-        def cast_values(h, c, copy):
-            copy(v_pool[h][:, c * CHUNK:(c + 1) * CHUNK], v_raw[h, c][:])
-
         def gather_values(h, b):
             nc.scalar.activation(
-                v_g[b][:, h, :].rearrange("p (g i t) -> p g t i", i=RUN, t=PACK),
+                v_g[h][:, b, :].rearrange("p (g i t) -> p g t i", i=RUN, t=PACK),
                 v_pool[h][:].indirect(seq_list(b)), ACT.Copy,
             )
 
-        cast_values(0, 0, nc.scalar.copy)
-        cast_values(0, 1, nc.scalar.copy)
-        qw = shared.tile([P, B, NQ], U32, name="qw", offset=v00_at, align_bytes=64)
-        nc.sync.dma_start(qw[:].bitcast(I32), q_words.rearrange("b o p q r -> p (b o) (q r)").bitcast(I32))
-        v_raw[1, 0] = raw_values("v_raw10", v10_at)
-        v_raw[1, 1] = raw_values("v_raw11", v01_at)
-        load_values(1, 0)
-        qs = shared.tile([P, B, NQ], U8, name="qs", offset=v00_at + B * NQ * 4, align_bytes=64)
-        nc.gpsimd.memset(qs[:].rearrange("p b q -> p (b q)").bitcast(I32), 0)
-        qs_rows = q_scales.bitcast(I32).rearrange("b o (a r) q -> r a (b o) q", r=4)
-        for r in range(4):
-            nc.sync.dma_start(qs[:].bitcast(I32)[r:P:32, :, :], qs_rows[r])
-        load_values(1, 1)
+        v_g = [sb.tile([P, B, N], BF16, name="v_g0")]
         gather_values(0, 0)
         gather_values(0, 1)
         cast_values(1, 0, nc.scalar.copy)
-        cast_values(1, 1, nc.vector.tensor_copy)
 
-        half_bytes = CHUNK_BYTES // 2
-        vs_g = [shared.tile([P, PACK, P], F32, name="vs_g%d" % b, offset=v01_at + b * half_bytes, align_bytes=64) for b in range(B)]
-        for b in range(B):
+        vs_g = []
+
+        def gather_scales(b, at):
+            vs_g.append(placed([P, PACK, P], F32, "vs_g%d" % b, at))
             nc.vector.tensor_copy(dealt(vs_g[b][:].bitcast(U32)), vs_pool[:].bitcast(U32).indirect(seq_list(b)))
 
+        gather_scales(0, kw_at)
+        cast_values(1, 1, nc.vector.tensor_copy)
+        gather_scales(1, v11_at)
+
         prob = [
-            shared.tile([P, PACK, NQ], F32, name="prob0", offset=v10_at, align_bytes=64),
+            placed([P, PACK, NQ], F32, "prob0", v10_at),
             sb.tile([P, PACK, NQ], F32, name="prob1", align_bytes=64),
         ]
         for b in range(B):
@@ -160,13 +175,14 @@ def tile_attend_sigm_kb_pgb2q256n512t2048_kernel(tc, q_words, q_scales, k_words,
             vs_bank.append(ps.tile([P, N], F32, name="vs_bank%d" % b, tag="bank%d" % (1 + b)))
             turn_rows(vs_bank[b], [vs_g[b][:, t, :] for t in reversed(range(PACK))])
 
+        v_g.append(sb.tile([P, B, N], BF16, name="v_g1", tag="kw_d1", align_bytes=64))
         gather_values(1, 0)
         gather_values(1, 1)
         v_bf = [sb.tile([P, DV * PACK], BF16, name="v_bf%d" % b, align_bytes=64) for b in range(B)]
         for b in range(B):
             bank = ps.tile([P, 2 * HALVES, P], F32, name="v_bank%d" % b, tag="bank%d" % (3 + b))
             for h in range(HALVES):
-                words = v_g[b][:, h, :].bitcast(F32)
+                words = v_g[h][:, b, :].bitcast(F32)
                 for u in range(2):
                     nc.tensor.transpose(bank[:, 2 * h + u, :], words[:, u:N // 2:2], ident[:])
             nc.scalar.copy(
@@ -174,7 +190,10 @@ def tile_attend_sigm_kb_pgb2q256n512t2048_kernel(tc, q_words, q_scales, k_words,
                 bank[:].rearrange("p (h u) e -> p h e u", u=2),
             )
 
-        w_bf = [sb.tile([P, NQ * PACK], BF16, name="w_bf%d" % b, align_bytes=64) for b in range(B)]
+        w_bf = [
+            placed([P, NQ * PACK], BF16, "w_bf0", v11_at + N * 4),
+            sb.tile([P, NQ * PACK], BF16, name="w_bf1", align_bytes=64),
+        ]
         v_codes = [sb.tile([P, DV], U32, name="v_codes%d" % b, align_bytes=64) for b in range(B)]
         v_sc = [sb.tile([P, DV], U8, name="v_sc%d" % b, align_bytes=64) for b in range(B)]
         w_codes = [sb.tile([P, NQ], U32, name="w_codes%d" % b, align_bytes=64) for b in range(B)]

@@ -101,7 +101,7 @@ def tile_attend_sigm_kb_pgb2q256n512t2048_kernel(tc, q_words, q_scales, k_words,
             return offsets[:, b * LIST_COLS:(b + 1) * LIST_COLS]
 
         def dealt(ap):
-            return ap.rearrange("p t (g i) -> p g t i", i=RUN)
+            return ap.rearrange("p (u e) (g i) -> p g u i e", i=RUN, e=2)
 
         def turn_rows(bank, rows):
             last = len(rows) - 1
@@ -120,8 +120,8 @@ def tile_attend_sigm_kb_pgb2q256n512t2048_kernel(tc, q_words, q_scales, k_words,
         nc.vector.tensor_copy(ks_g[:], ks_pool[:].indirect(offsets[:]))
         ks_d = sb.tile([P, PACK, B * P], U8, name="ks_d", align_bytes=64)
         nc.vector.tensor_copy(
-            ks_d[:].bitcast(I32).rearrange("p t (g w) -> p g t w", w=2),
-            ks_g[:].bitcast(I32).rearrange("p (g t w) -> p g t w", t=PACK, w=2),
+            ks_d[:].rearrange("p (u e) (g i) -> p g u e i", i=RUN, e=2),
+            ks_g[:].rearrange("p (g u i e) -> p g u e i", u=2, i=RUN, e=2),
         )
         kb_col = sb.tile([P, B * PACK], F32, name="kb_col", tag="ks_g")
         nc.vector.tensor_copy(kb_col[:], kb_bank[:, ROW:ROW + B * PACK * TURN_STEP:TURN_STEP])
@@ -131,7 +131,7 @@ def tile_attend_sigm_kb_pgb2q256n512t2048_kernel(tc, q_words, q_scales, k_words,
 
         def gather_values(h, b):
             nc.scalar.activation(
-                v_g[h][:, b, :].rearrange("p (g i t) -> p g t i", i=RUN, t=PACK),
+                v_g[h][:, b, :].rearrange("p (u g k) -> p g u k", u=2, k=2 * RUN),
                 v_pool[h][:].indirect(seq_list(b)), ACT.Copy,
             )
 
@@ -184,7 +184,7 @@ def tile_attend_sigm_kb_pgb2q256n512t2048_kernel(tc, q_words, q_scales, k_words,
             for h in range(HALVES):
                 words = v_g[h][:, b, :].bitcast(F32)
                 for u in range(2):
-                    nc.tensor.transpose(bank[:, 2 * h + u, :], words[:, u:N // 2:2], ident[:])
+                    nc.tensor.transpose(bank[:, 2 * h + u, :], words[:, u * P:(u + 1) * P], ident[:])
             nc.scalar.copy(
                 v_bf[b][:].bitcast(F32).rearrange("p (h e u) -> p h e u", h=HALVES, u=2),
                 bank[:].rearrange("p (h u) e -> p h e u", u=2),

@@ -41,24 +41,27 @@ def tile_attend_sigm_kb_pgb2q256n512t2048_kernel(tc, q_words, q_scales, k_words,
         ident = sb.tile([P, P], F32, name="ident")
 
         warm = sb.tile([P, 2], F32, name="warm")
-        nc.vector.memset(warm[:, 0:1], 0.0)
         nc.vector.memset(ks_pool[:].bitcast(I32), 0)
-        nc.vector.memset(kb_pool[0:ROW, :], 0.0)
+        qs = sb.tile([P, B, NQ], U8, name="qs", align_bytes=64)
+        nc.vector.memset(qs[:].rearrange("p b q -> p (b q)").bitcast(I32), 0)
+        nc.vector.memset(warm[:, 0:1], 0.0)
+        nc.vector.memset(kb_pool[0:ROW, 0:CHUNK], 0.0)
+        nc.gpsimd.memset(kb_pool[0:ROW, CHUNK:T], 0.0)
         make_identity(nc, ident[:])
         nc.scalar.activation(warm[:, 1:2], warm[:, 0:1], ACT.Sigmoid)
 
         def placed(shape, dtype, name, at):
             return shared.tile(shape, dtype, name=name, tag="at%d" % at, offset=at, align_bytes=64)
 
-        cols = {(0, 0): (0, FIRST), (0, 1): (FIRST, T), (1, 0): (0, CHUNK), (1, 1): (CHUNK, T)}
+        cols = {(0, 0): (0, FIRST), (0, 1): (FIRST, T - FIRST), (0, 2): (T - FIRST, T), (1, 0): (0, CHUNK), (1, 1): (CHUNK, T)}
         kw_at = 0
-        v00_at = kw_at + T * 4 - LAP
-        qs_at = v00_at + LAP
-        v10_at = v00_at + FIRST * 4 - LAP
-        v01_at = v10_at + CHUNK * 4
-        qw_at = v01_at
-        v11_at = v01_at + (T - FIRST) * 4 - LAP
-        v_at = {(0, 0): v00_at, (0, 1): v01_at, (1, 0): v10_at, (1, 1): v11_at}
+        v00_at = kw_at + T * 4
+        v10_at = v00_at + FIRST * 4
+        vs_at = v10_at + CHUNK * 4
+        v01_at = vs_at + T * 4 - LAP
+        v11_at = v01_at + CHUNK * 4
+        v02_at = v11_at + CHUNK * 4
+        v_at = {(0, 0): v00_at, (0, 1): v01_at, (0, 2): v02_at, (1, 0): v10_at, (1, 1): v11_at}
         v_raw = {}
 
         def load_values(h, c):
@@ -70,9 +73,7 @@ def tile_attend_sigm_kb_pgb2q256n512t2048_kernel(tc, q_words, q_scales, k_words,
         nc.sync.dma_start(kb_pool[ROW:P, :], kb[0:1, :])
         load_values(0, 0)
         load_values(0, 1)
-        vs_pool = sb.tile([P, T], F32, name="vs_pool")
-        nc.sync.dma_start(vs_pool[ROW:P, :], vs[0:1, :])
-        nc.gpsimd.memset(vs_pool[0:ROW, :], 0.0)
+        load_values(0, 2)
         ks_rows = k_scales[0].bitcast(I32).rearrange("(a r) t -> r a t", r=4)
         for r in range(4):
             nc.sync.dma_start(ks_pool[:].bitcast(I32)[r:P:32, :], ks_rows[r])
@@ -87,13 +88,15 @@ def tile_attend_sigm_kb_pgb2q256n512t2048_kernel(tc, q_words, q_scales, k_words,
         kw_pool = placed([P, T], U32, "kw_pool", kw_at)
         nc.sync.dma_start(kw_pool[:].bitcast(I32), k_words[0].rearrange("p t r -> p (t r)").bitcast(I32))
         load_values(1, 0)
-        qs = placed([P, B, NQ], U8, "qs", qs_at)
-        nc.gpsimd.memset(qs[:].rearrange("p b q -> p (b q)").bitcast(I32), 0)
         qs_rows = q_scales.bitcast(I32).rearrange("b o (a r) q -> r a (b o) q", r=4)
         for r in range(4):
             nc.sync.dma_start(qs[:].bitcast(I32)[r:P:32, :, :], qs_rows[r])
         cast_values(0, 1, nc.scalar.copy)
-        qw = placed([P, B, NQ], U32, "qw", qw_at)
+        cast_values(0, 2, nc.scalar.copy)
+        vs_pool = placed([P, T], F32, "vs_pool", vs_at)
+        nc.sync.dma_start(vs_pool[ROW:P, :], vs[0:1, :])
+        nc.gpsimd.memset(vs_pool[0:ROW, :], 0.0)
+        qw = sb.tile([P, B, NQ], U32, name="qw", align_bytes=64)
         nc.sync.dma_start(qw[:].bitcast(I32), q_words.rearrange("b o p q r -> p (b o) (q r)").bitcast(I32))
         load_values(1, 1)
 
@@ -123,8 +126,6 @@ def tile_attend_sigm_kb_pgb2q256n512t2048_kernel(tc, q_words, q_scales, k_words,
             ks_d[:].rearrange("p (u e) (g i) -> p g u e i", i=RUN, e=2),
             ks_g[:].rearrange("p (g u i e) -> p g u e i", u=2, i=RUN, e=2),
         )
-        kb_col = sb.tile([P, B * PACK], F32, name="kb_col", tag="ks_g")
-        nc.vector.tensor_copy(kb_col[:], kb_bank[:, ROW:ROW + B * PACK * TURN_STEP:TURN_STEP])
         kw_d = [sb.tile([P, PACK, P], U32, name="kw_d%d" % b, tag="kw_d%d" % b, align_bytes=64) for b in range(B)]
         for b in range(B):
             nc.vector.tensor_copy(dealt(kw_d[b][:]), kw_pool[:].indirect(seq_list(b)))
@@ -138,6 +139,8 @@ def tile_attend_sigm_kb_pgb2q256n512t2048_kernel(tc, q_words, q_scales, k_words,
         v_g = [sb.tile([P, B, N], BF16, name="v_g0")]
         gather_values(0, 0)
         gather_values(0, 1)
+        kb_col = placed([P, B * PACK], F32, "kb_col", v02_at)
+        nc.scalar.copy(kb_col[:], kb_bank[:, ROW:ROW + B * PACK * TURN_STEP:TURN_STEP])
         cast_values(1, 0, nc.scalar.copy)
 
         vs_g = []
@@ -146,7 +149,7 @@ def tile_attend_sigm_kb_pgb2q256n512t2048_kernel(tc, q_words, q_scales, k_words,
             vs_g.append(placed([P, PACK, P], F32, "vs_g%d" % b, at))
             nc.vector.tensor_copy(dealt(vs_g[b][:].bitcast(U32)), vs_pool[:].bitcast(U32).indirect(seq_list(b)))
 
-        gather_scales(0, kw_at)
+        gather_scales(0, v02_at + FIRST * 4)
         cast_values(1, 1, nc.vector.tensor_copy)
         gather_scales(1, v11_at)
 

@@ -151,7 +151,7 @@ def tile_attend_sigm_kb_pgb2q256n512t2048_kernel(tc, q_words, q_scales, k_words,
 
         gather_scales(0, v02_at + FIRST * 4)
         cast_values(1, 1, nc.vector.tensor_copy)
-        gather_scales(1, v11_at)
+        gather_scales(1, v11_at + LAP)
 
         prob = [
             placed([P, PACK, NQ], F32, "prob0", v10_at),
@@ -194,7 +194,7 @@ def tile_attend_sigm_kb_pgb2q256n512t2048_kernel(tc, q_words, q_scales, k_words,
             )
 
         w_bf = [
-            placed([P, NQ * PACK], BF16, "w_bf0", v11_at + N * 4),
+            placed([P, NQ * PACK], BF16, "w_bf0", v11_at + LAP - N * 4),
             sb.tile([P, NQ * PACK], BF16, name="w_bf1", align_bytes=64),
         ]
         v_codes = [sb.tile([P, DV], U32, name="v_codes%d" % b, align_bytes=64) for b in range(B)]

@@ -22,7 +22,6 @@ RUN = 8
 ROW = P - 1
 HALVES = DV // P
 CHUNK = T // 2
-FIRST = 512
 LAP = 64
 LIST_COLS = N // 16
 TURN_STEP = 8
@@ -53,15 +52,14 @@ def tile_attend_sigm_kb_pgb2q256n512t2048_kernel(tc, q_words, q_scales, k_words,
         def placed(shape, dtype, name, at):
             return shared.tile(shape, dtype, name=name, tag="at%d" % at, offset=at, align_bytes=64)
 
-        cols = {(0, 0): (0, FIRST), (0, 1): (FIRST, T - FIRST), (0, 2): (T - FIRST, T), (1, 0): (0, CHUNK), (1, 1): (CHUNK, T)}
+        cols = {(0, 0): (0, CHUNK), (0, 1): (CHUNK, T), (1, 0): (0, CHUNK), (1, 1): (CHUNK, T)}
         kw_at = 0
-        v00_at = kw_at + T * 4
-        v10_at = v00_at + FIRST * 4
+        v10_at = kw_at + T * 4
         vs_at = v10_at + CHUNK * 4
-        v01_at = vs_at + T * 4 - LAP
-        v11_at = v01_at + CHUNK * 4
-        v02_at = v11_at + CHUNK * 4
-        v_at = {(0, 0): v00_at, (0, 1): v01_at, (0, 2): v02_at, (1, 0): v10_at, (1, 1): v11_at}
+        v00_at = vs_at + T * 4 - LAP
+        v11_at = v00_at + CHUNK * 4
+        v01_at = v11_at + CHUNK * 4
+        v_at = {(0, 0): v00_at, (0, 1): v01_at, (1, 0): v10_at, (1, 1): v11_at}
         v_raw = {}
 
         def load_values(h, c):
@@ -73,7 +71,6 @@ def tile_attend_sigm_kb_pgb2q256n512t2048_kernel(tc, q_words, q_scales, k_words,
         nc.sync.dma_start(kb_pool[ROW:P, :], kb[0:1, :])
         load_values(0, 0)
         load_values(0, 1)
-        load_values(0, 2)
         ks_rows = k_scales[0].bitcast(I32).rearrange("(a r) t -> r a t", r=4)
         for r in range(4):
             nc.sync.dma_start(ks_pool[:].bitcast(I32)[r:P:32, :], ks_rows[r])
@@ -92,7 +89,6 @@ def tile_attend_sigm_kb_pgb2q256n512t2048_kernel(tc, q_words, q_scales, k_words,
         for r in range(4):
             nc.sync.dma_start(qs[:].bitcast(I32)[r:P:32, :, :], qs_rows[r])
         cast_values(0, 1, nc.scalar.copy)
-        cast_values(0, 2, nc.scalar.copy)
         vs_pool = placed([P, T], F32, "vs_pool", vs_at)
         nc.sync.dma_start(vs_pool[ROW:P, :], vs[0:1, :])
         nc.gpsimd.memset(vs_pool[0:ROW, :], 0.0)
@@ -139,7 +135,7 @@ def tile_attend_sigm_kb_pgb2q256n512t2048_kernel(tc, q_words, q_scales, k_words,
         v_g = [sb.tile([P, B, N], BF16, name="v_g0")]
         gather_values(0, 0)
         gather_values(0, 1)
-        kb_col = placed([P, B * PACK], F32, "kb_col", v02_at)
+        kb_col = placed([P, B * PACK], F32, "kb_col", v01_at)
         nc.scalar.copy(kb_col[:], kb_bank[:, ROW:ROW + B * PACK * TURN_STEP:TURN_STEP])
         cast_values(1, 0, nc.scalar.copy)
 
@@ -149,7 +145,7 @@ def tile_attend_sigm_kb_pgb2q256n512t2048_kernel(tc, q_words, q_scales, k_words,
             vs_g.append(placed([P, PACK, P], F32, "vs_g%d" % b, at))
             nc.vector.tensor_copy(dealt(vs_g[b][:].bitcast(U32)), vs_pool[:].bitcast(U32).indirect(seq_list(b)))
 
-        gather_scales(0, v02_at + FIRST * 4)
+        gather_scales(0, v01_at + CHUNK * 4)
         cast_values(1, 1, nc.vector.tensor_copy)
         gather_scales(1, v11_at + LAP)
 

@@ -18,11 +18,8 @@ ALU = mybir.AluOpType
 
 P = 128
 PACK = 4
-RUN = 8
 ROW = P - 1
 HALVES = DV // P
-CHUNK = T // 2
-LAP = 64
 LIST_COLS = N // 16
 TURN_STEP = 8
 
@@ -34,201 +31,156 @@ def tile_attend_sigm_kb_pgb2q256n512t2048_kernel(tc, q_words, q_scales, k_words,
         shared = ctx.enter_context(tc.tile_pool(name="shared", bufs=1))
         ps = ctx.enter_context(tc.psum_pool(name="ps", bufs=1))
 
+        def placed(shape, dtype, name, at):
+            return shared.tile(shape, dtype, name=name, tag=name, offset=at, align_bytes=64)
+
+        def bank(shape, name, n):
+            return ps.tile(shape, F32, name=name, tag="bank%d" % n)
+
+        vs_at = 0
+        v0_at = vs_at + T * 4
+
         offsets = sb.tile([P, B * LIST_COLS], U16, name="offsets")
         kb_pool = sb.tile([P, T], F32, name="kb_pool")
+        vs_pool = placed([P, T], F32, "vs_pool", vs_at)
         ks_pool = sb.tile([P, T], U8, name="ks_pool")
+        kw_pool = sb.tile([P, T], U32, name="kw_pool")
         ident = sb.tile([P, P], F32, name="ident")
-
-        warm = sb.tile([P, 2], F32, name="warm")
-        nc.vector.memset(ks_pool[:].bitcast(I32), 0)
         qs = sb.tile([P, B, NQ], U8, name="qs", align_bytes=64)
+        qw = sb.tile([P, B, NQ], U32, name="qw", align_bytes=64)
+        warm = sb.tile([P, 2], F32, name="warm")
+
+        nc.gpsimd.memset(ks_pool[:].bitcast(I32), 0)
         nc.vector.memset(qs[:].rearrange("p b q -> p (b q)").bitcast(I32), 0)
         nc.vector.memset(warm[:, 0:1], 0.0)
-        nc.vector.memset(kb_pool[0:ROW, 0:CHUNK], 0.0)
-        nc.gpsimd.memset(kb_pool[0:ROW, CHUNK:T], 0.0)
+        nc.vector.memset(kb_pool[0:ROW, 0:T * 3 // 4], 0.0)
+        nc.gpsimd.memset(kb_pool[0:ROW, T * 3 // 4:T], 0.0)
         make_identity(nc, ident[:])
+        nc.gpsimd.memset(vs_pool[0:ROW, :], 0.0)
         nc.scalar.activation(warm[:, 1:2], warm[:, 0:1], ACT.Sigmoid)
-
-        def placed(shape, dtype, name, at):
-            return shared.tile(shape, dtype, name=name, tag="at%d" % at, offset=at, align_bytes=64)
-
-        cols = {(0, 0): (0, CHUNK), (0, 1): (CHUNK, T), (1, 0): (0, CHUNK), (1, 1): (CHUNK, T)}
-        kw_at = 0
-        v10_at = kw_at + T * 4
-        vs_at = v10_at + CHUNK * 4
-        v00_at = vs_at + T * 4 - LAP
-        v11_at = v00_at + CHUNK * 4
-        v01_at = v11_at + CHUNK * 4
-        v_at = {(0, 0): v00_at, (0, 1): v01_at, (1, 0): v10_at, (1, 1): v11_at}
-        v_raw = {}
-
-        def load_values(h, c):
-            lo, hi = cols[h, c]
-            v_raw[h, c] = placed([P, hi - lo], F32, "v_raw%d%d" % (h, c), v_at[h, c])
-            nc.sync.dma_start(v_raw[h, c][:], vT[h * P:(h + 1) * P, lo:hi])
 
         nc.sync.dma_start(offsets[:], offs)
         nc.sync.dma_start(kb_pool[ROW:P, :], kb[0:1, :])
-        load_values(0, 0)
-        load_values(0, 1)
+        nc.sync.dma_start(vs_pool[ROW:P, :], vs[0:1, :])
         ks_rows = k_scales[0].bitcast(I32).rearrange("(a r) t -> r a t", r=4)
         for r in range(4):
             nc.sync.dma_start(ks_pool[:].bitcast(I32)[r:P:32, :], ks_rows[r])
-
-        v_pool = [sb.tile([P, T], BF16, name="v_pool%d" % h) for h in range(HALVES)]
-
-        def cast_values(h, c, copy):
-            lo, hi = cols[h, c]
-            copy(v_pool[h][:, lo:hi], v_raw[h, c][:])
-
-        cast_values(0, 0, nc.scalar.copy)
-        kw_pool = placed([P, T], U32, "kw_pool", kw_at)
         nc.sync.dma_start(kw_pool[:].bitcast(I32), k_words[0].rearrange("p t r -> p (t r)").bitcast(I32))
-        load_values(1, 0)
+        nc.sync.dma_start(qw[:].bitcast(I32), q_words.rearrange("b o p q r -> p (b o) (q r)").bitcast(I32))
         qs_rows = q_scales.bitcast(I32).rearrange("b o (a r) q -> r a (b o) q", r=4)
         for r in range(4):
             nc.sync.dma_start(qs[:].bitcast(I32)[r:P:32, :, :], qs_rows[r])
-        cast_values(0, 1, nc.scalar.copy)
-        vs_pool = placed([P, T], F32, "vs_pool", vs_at)
-        nc.sync.dma_start(vs_pool[ROW:P, :], vs[0:1, :])
-        nc.gpsimd.memset(vs_pool[0:ROW, :], 0.0)
-        qw = sb.tile([P, B, NQ], U32, name="qw", align_bytes=64)
-        nc.sync.dma_start(qw[:].bitcast(I32), q_words.rearrange("b o p q r -> p (b o) (q r)").bitcast(I32))
-        load_values(1, 1)
+        v_pool = [placed([P, T], F32, "v_pool%d" % h, v0_at + h * T * 4) for h in range(HALVES)]
+        for h in range(HALVES):
+            nc.sync.dma_start(v_pool[h][:], vT[h * P:(h + 1) * P, :])
 
         def seq_list(b):
             return offsets[:, b * LIST_COLS:(b + 1) * LIST_COLS]
 
-        def dealt(ap):
-            return ap.rearrange("p (u e) (g i) -> p g u i e", i=RUN, e=2)
-
-        def turn_rows(bank, rows):
-            last = len(rows) - 1
-            cols = []
-            for n, row in enumerate(rows):
-                at = (last - n) * TURN_STEP
-                nc.tensor.transpose(bank[:, at:at + P], row, ident[:])
-                cols.append(at + ROW)
-            return cols
-
-        kb_g = sb.tile([P, PACK, B * P], F32, name="kb_g")
-        nc.vector.tensor_copy(dealt(kb_g[:].bitcast(U32)), kb_pool[:].bitcast(U32).indirect(offsets[:]))
-        kb_bank = ps.tile([P, N], F32, name="kb_bank", tag="bank0")
-        turn_rows(kb_bank, [kb_g[:, t, b * P:(b + 1) * P] for b in reversed(range(B)) for t in reversed(range(PACK))])
-        ks_g = sb.tile([P, B * N], U8, name="ks_g", tag="ks_g")
-        nc.vector.tensor_copy(ks_g[:], ks_pool[:].indirect(offsets[:]))
-        ks_d = sb.tile([P, PACK, B * P], U8, name="ks_d", align_bytes=64)
-        nc.vector.tensor_copy(
-            ks_d[:].rearrange("p (u e) (g i) -> p g u e i", i=RUN, e=2),
-            ks_g[:].rearrange("p (g u i e) -> p g u e i", u=2, i=RUN, e=2),
-        )
-        kw_d = [sb.tile([P, PACK, P], U32, name="kw_d%d" % b, tag="kw_d%d" % b, align_bytes=64) for b in range(B)]
+        ks_d = sb.tile([P, B, PACK, P], U8, name="ks_d", align_bytes=64)
+        nc.vector.tensor_copy(ks_d[:].rearrange("p b t s -> p b s t"), ks_pool[:].indirect(offsets[:]))
+        kw_d = [sb.tile([P, PACK, P], U32, name="kw_d%d" % b, align_bytes=64) for b in range(B)]
         for b in range(B):
-            nc.vector.tensor_copy(dealt(kw_d[b][:]), kw_pool[:].indirect(seq_list(b)))
+            nc.vector.tensor_copy(kw_d[b][:].rearrange("p t s -> p s t"), kw_pool[:].indirect(seq_list(b)))
 
-        def gather_values(h, b):
-            nc.scalar.activation(
-                v_g[h][:, b, :].rearrange("p (u g k) -> p g u k", u=2, k=2 * RUN),
-                v_pool[h][:].indirect(seq_list(b)), ACT.Copy,
-            )
+        def gather_row(pool, name, b):
+            row = sb.tile([P, N], F32, name="%s%d" % (name, b))
+            nc.scalar.activation(row[:], pool[:].indirect(seq_list(b)), ACT.Copy)
+            return row
 
-        v_g = [sb.tile([P, B, N], BF16, name="v_g0")]
-        gather_values(0, 0)
-        gather_values(0, 1)
-        kb_col = placed([P, B * PACK], F32, "kb_col", v01_at)
+        def turn_row(dst, places, first):
+            for t in reversed(range(PACK)):
+                at = (first + t) * TURN_STEP
+                nc.tensor.transpose(dst[:, at:at + P], places[t], ident[:])
+
+        def stepped(row):
+            return [row[:, t:N:PACK] for t in range(PACK)]
+
+        kb_g = [gather_row(kb_pool, "kb_g", b) for b in reversed(range(B))]
+        vs_g = [gather_row(vs_pool, "vs_g", b) for b in range(B)]
+        kb_bank = bank([P, N], "kb_bank", 0)
+        for n, b in enumerate(reversed(range(B))):
+            turn_row(kb_bank, stepped(kb_g[n]), b * PACK)
+        kb_col = placed([P, B * PACK], F32, "kb_col", vs_at)
         nc.scalar.copy(kb_col[:], kb_bank[:, ROW:ROW + B * PACK * TURN_STEP:TURN_STEP])
-        cast_values(1, 0, nc.scalar.copy)
 
-        vs_g = []
-
-        def gather_scales(b, at):
-            vs_g.append(placed([P, PACK, P], F32, "vs_g%d" % b, at))
-            nc.vector.tensor_copy(dealt(vs_g[b][:].bitcast(U32)), vs_pool[:].bitcast(U32).indirect(seq_list(b)))
-
-        gather_scales(0, v01_at + CHUNK * 4)
-        cast_values(1, 1, nc.vector.tensor_copy)
-        gather_scales(1, v11_at + LAP)
-
-        prob = [
-            placed([P, PACK, NQ], F32, "prob0", v10_at),
-            sb.tile([P, PACK, NQ], F32, name="prob1", align_bytes=64),
-        ]
+        prob = [sb.tile([P, PACK, NQ], F32, name="prob%d" % b, align_bytes=64) for b in range(B)]
         for b in range(B):
             for half in range(2):
-                bank = ps.tile([P, 2, NQ], F32, name="score%d%d" % (b, half), tag="bank%d" % (1 + 2 * b + half))
+                score = bank([P, 2, NQ], "score%d%d" % (b, half), 1 + 2 * b + half)
                 for u in range(2):
                     t = 2 * half + u
                     nc.tensor.matmul_mx(
-                        out=bank[:, u, :],
-                        lhsT=kw_d[b][:, t, :].bitcast(FP8X4), lhsT_scale=ks_d[:, t, b * P:(b + 1) * P],
+                        out=score[:, u, :],
+                        lhsT=kw_d[b][:, t, :].bitcast(FP8X4), lhsT_scale=ks_d[:, b, t, :],
                         rhs=qw[:, b, :].bitcast(FP8X4), rhs_scale=qs[:, b, :],
                         start=True, stop=True,
                     )
                 for u in range(2):
                     t = 2 * half + u
                     c = b * PACK + t
-                    nc.scalar.activation(prob[b][:, t, :], bank[:, u, :], ACT.Sigmoid, bias=kb_col[:, c:c + 1])
+                    nc.scalar.activation(prob[b][:, t, :], score[:, u, :], ACT.Sigmoid, bias=kb_col[:, c:c + 1])
 
-        vs_bank = []
+        vs_bank = [bank([P, N], "vs_bank%d" % b, 1 + b) for b in range(B)]
         for b in range(B):
-            vs_bank.append(ps.tile([P, N], F32, name="vs_bank%d" % b, tag="bank%d" % (1 + b)))
-            turn_rows(vs_bank[b], [vs_g[b][:, t, :] for t in reversed(range(PACK))])
+            turn_row(vs_bank[b], stepped(vs_g[b]), 0)
 
-        v_g.append(sb.tile([P, B, N], BF16, name="v_g1", tag="kw_d1", align_bytes=64))
-        gather_values(1, 0)
-        gather_values(1, 1)
-        v_bf = [sb.tile([P, DV * PACK], BF16, name="v_bf%d" % b, align_bytes=64) for b in range(B)]
-        for b in range(B):
-            bank = ps.tile([P, 2 * HALVES, P], F32, name="v_bank%d" % b, tag="bank%d" % (3 + b))
-            for h in range(HALVES):
-                words = v_g[h][:, b, :].bitcast(F32)
-                for u in range(2):
-                    nc.tensor.transpose(bank[:, 2 * h + u, :], words[:, u * P:(u + 1) * P], ident[:])
-            nc.scalar.copy(
-                v_bf[b][:].bitcast(F32).rearrange("p (h e u) -> p h e u", h=HALVES, u=2),
-                bank[:].rearrange("p (h u) e -> p h e u", u=2),
-            )
+        def gather_values(h, b, on_vector):
+            v_g = sb.tile([P, N], BF16, name="v_g%d%d" % (h, b), align_bytes=64)
+            window = v_pool[h][:].indirect(seq_list(b))
+            if on_vector:
+                nc.vector.tensor_copy(v_g[:], window)
+            else:
+                nc.scalar.activation(v_g[:], window, ACT.Copy)
+            words = v_g[:].bitcast(F32)
+            for u in range(2):
+                nc.tensor.transpose(v_bank[b][:, h, u, :], words[:, u:N // 2:2], ident[:])
 
-        w_bf = [
-            placed([P, NQ * PACK], BF16, "w_bf0", v11_at + LAP - N * 4),
-            sb.tile([P, NQ * PACK], BF16, name="w_bf1", align_bytes=64),
-        ]
-        v_codes = [sb.tile([P, DV], U32, name="v_codes%d" % b, align_bytes=64) for b in range(B)]
-        v_sc = [sb.tile([P, DV], U8, name="v_sc%d" % b, align_bytes=64) for b in range(B)]
-        w_codes = [sb.tile([P, NQ], U32, name="w_codes%d" % b, align_bytes=64) for b in range(B)]
-        w_sc = [sb.tile([P, NQ], U8, name="w_sc%d" % b, align_bytes=64) for b in range(B)]
+        def weave_values(b, copy):
+            v_bf = sb.tile([P, DV * PACK], BF16, name="v_bf%d" % b, align_bytes=64)
+            copy(v_bf[:].bitcast(F32).rearrange("p (h e u) -> p h e u", e=P, u=2), v_bank[b][:].rearrange("p h u e -> p h e u"))
+            return v_bf
+
+        def quantize(name, values):
+            codes = sb.tile([P, NQ], U32, name=name + "_codes", align_bytes=64)
+            scales = sb.tile([P, NQ], U8, name=name + "_scales", align_bytes=64)
+            nc.vector.quantize_mx(out=codes[:].bitcast(FP8X4), scales=scales[:], in_=values[:])
+            return codes, scales
 
         def weigh(b):
+            w_bf = placed([P, NQ * PACK], BF16, "w_bf%d" % b, v0_at + b * NQ * PACK * 2)
             scale = vs_bank[b][:, ROW:ROW + PACK * TURN_STEP:TURN_STEP].unsqueeze(1).unsqueeze(3).to_broadcast([P, NQ // 4, PACK, 4])
             nc.vector.tensor_tensor(
-                w_bf[b][:].rearrange("p (c i t) -> p c t i", i=4, t=PACK),
+                w_bf[:].rearrange("p (c i t) -> p c t i", i=4, t=PACK),
                 prob[b][:].rearrange("p t (c i) -> p c t i", i=4),
                 scale, ALU.mult,
             )
+            return w_bf
 
-        def quantize(codes, scales, values):
-            nc.vector.quantize_mx(out=codes[:].bitcast(FP8X4), scales=scales[:], in_=values[:])
-
-        def finish(b, m):
+        def finish(b, m, w_q, v_q, n, on_vector):
+            acc = bank([P, DV], "acc%d%d" % (b, m), n)
             rows = slice(m * P, (m + 1) * P)
-            acc = ps.tile([P, N], F32, name="acc%d%d" % (b, m), tag="bank%d" % (0, 5, 6, 7)[2 * b + m])
             nc.tensor.matmul_mx(
-                out=acc[:, 0:DV],
-                lhsT=w_codes[b][:, rows].bitcast(FP8X4), lhsT_scale=w_sc[b][:, rows],
-                rhs=v_codes[b][:].bitcast(FP8X4), rhs_scale=v_sc[b][:],
+                out=acc[:],
+                lhsT=w_q[0][:, rows].bitcast(FP8X4), lhsT_scale=w_q[1][:, rows],
+                rhs=v_q[0][:].bitcast(FP8X4), rhs_scale=v_q[1][:],
                 start=True, stop=True,
             )
             y = sb.tile([P, DV], F32, name="y%d%d" % (b, m))
-            if (b, m) == (1, 1):
-                nc.vector.tensor_scalar(y[:], acc[:, 0:DV], 1.0 / 16.0, None, ALU.mult)
+            if on_vector:
+                nc.vector.tensor_scalar(y[:], acc[:], 1.0 / 16.0, None, ALU.mult)
             else:
-                nc.scalar.activation(y[:], acc[:, 0:DV], ACT.Copy, scale=1.0 / 16.0)
+                nc.scalar.activation(y[:], acc[:], ACT.Copy, scale=1.0 / 16.0)
             nc.sync.dma_start(out[b, rows, :], y[:])
 
-        weigh(0)
-        weigh(1)
+        v_bank = [bank([P, HALVES, 2, P], "v_bank%d" % b, 3 + b) for b in range(B)]
+        for h in range(HALVES):
+            for b in range(B):
+                gather_values(h, b, h == 0)
+        w_bf = [weigh(b) for b in range(B)]
+        w_q = [quantize("w%d" % b, w_bf[b]) for b in range(B)]
+        v_bf = [weave_values(b, nc.scalar.copy) for b in range(B)]
+        v_q = [quantize("v%d" % b, v_bf[b]) for b in range(B)]
         for b in range(B):
-            quantize(w_codes[b], w_sc[b], w_bf[b])
-            quantize(v_codes[b], v_sc[b], v_bf[b])
-            finish(b, 0)
-            finish(b, 1)
+            for m in range(2):
+                finish(b, m, w_q[b], v_q[b], (5, 6, 7, 0)[2 * b + m], (b, m) == (1, 0))

@@ -62,11 +62,11 @@ def tile_attend_sigm_kb_pgb2q256n512t2048_kernel(tc, q_words, q_scales, k_words,
         nc.sync.dma_start(offsets[:], offs)
         nc.sync.dma_start(kb_pool[ROW:P, :], kb[0:1, :])
         nc.sync.dma_start(vs_pool[ROW:P, :], vs[0:1, :])
+        nc.sync.dma_start(qw[:].bitcast(I32), q_words.rearrange("b o p q r -> p (b o) (q r)").bitcast(I32))
         ks_rows = k_scales[0].bitcast(I32).rearrange("(a r) t -> r a t", r=4)
         for r in range(4):
             nc.sync.dma_start(ks_pool[:].bitcast(I32)[r:P:32, :], ks_rows[r])
         nc.sync.dma_start(kw_pool[:].bitcast(I32), k_words[0].rearrange("p t r -> p (t r)").bitcast(I32))
-        nc.sync.dma_start(qw[:].bitcast(I32), q_words.rearrange("b o p q r -> p (b o) (q r)").bitcast(I32))
         qs_rows = q_scales.bitcast(I32).rearrange("b o (a r) q -> r a (b o) q", r=4)
         for r in range(4):
             nc.sync.dma_start(qs[:].bitcast(I32)[r:P:32, :, :], qs_rows[r])

@@ -53,7 +53,8 @@ def tile_attend_sigm_kb_pgb2q256n512t2048_kernel(tc, q_words, q_scales, k_words,
         nc.gpsimd.memset(ks_pool[:].bitcast(I32), 0)
         nc.vector.memset(qs[:].rearrange("p b q -> p (b q)").bitcast(I32), 0)
         nc.vector.memset(warm[:, 0:1], 0.0)
-        nc.vector.memset(kb_pool[0:ROW, 0:T * 3 // 4], 0.0)
+        nc.vector.memset(kb_pool[0:ROW, 0:T * 3 // 4 - 1], 0.0)
+        nc.vector.memset(kb_pool[0:ROW, T * 3 // 4 - 1:T * 3 // 4], 0.0)
         nc.gpsimd.memset(kb_pool[0:ROW, T * 3 // 4:T], 0.0)
         make_identity(nc, ident[:])
         nc.gpsimd.memset(vs_pool[0:ROW, :], 0.0)

@@ -22,6 +22,7 @@ ROW = P - 1
 HALVES = DV // P
 LIST_COLS = N // 16
 TURN_STEP = 8
+SHARE = T * 3 // 4
 
 
 def tile_attend_sigm_kb_pgb2q256n512t2048_kernel(tc, q_words, q_scales, k_words, k_scales, vT, vs, kb, offs, out):
@@ -39,9 +40,10 @@ def tile_attend_sigm_kb_pgb2q256n512t2048_kernel(tc, q_words, q_scales, k_words,
 
         vs_at = 0
         v0_at = vs_at + T * 4
+        kb_at = v0_at + HALVES * T * 4
 
         offsets = sb.tile([P, B * LIST_COLS], U16, name="offsets")
-        kb_pool = sb.tile([P, T], F32, name="kb_pool")
+        kb_pool = placed([P, T], F32, "kb_pool", kb_at)
         vs_pool = placed([P, T], F32, "vs_pool", vs_at)
         ks_pool = sb.tile([P, T], U8, name="ks_pool")
         kw_pool = sb.tile([P, T], U32, name="kw_pool")
@@ -53,16 +55,18 @@ def tile_attend_sigm_kb_pgb2q256n512t2048_kernel(tc, q_words, q_scales, k_words,
         nc.gpsimd.memset(ks_pool[:].bitcast(I32), 0)
         nc.vector.memset(qs[:].rearrange("p b q -> p (b q)").bitcast(I32), 0)
         nc.vector.memset(warm[:, 0:1], 0.0)
-        nc.vector.memset(kb_pool[0:ROW, 0:T * 3 // 4 - 1], 0.0)
-        nc.vector.memset(kb_pool[0:ROW, T * 3 // 4 - 1:T * 3 // 4], 0.0)
-        nc.gpsimd.memset(kb_pool[0:ROW, T * 3 // 4:T], 0.0)
+        nc.vector.memset(vs_pool[0:ROW, 0:SHARE - 1], 0.0)
+        nc.vector.memset(vs_pool[0:ROW, SHARE - 1:SHARE], 0.0)
+        nc.gpsimd.memset(vs_pool[0:ROW, SHARE:T], 0.0)
+        nc.vector.memset(kb_pool[0:ROW, 0:T - SHARE - 1], 0.0)
+        nc.vector.memset(kb_pool[0:ROW, T - SHARE - 1:T - SHARE], 0.0)
+        nc.gpsimd.memset(kb_pool[0:ROW, T - SHARE:T], 0.0)
         make_identity(nc, ident[:])
-        nc.gpsimd.memset(vs_pool[0:ROW, :], 0.0)
         nc.scalar.activation(warm[:, 1:2], warm[:, 0:1], ACT.Sigmoid)
 
         nc.sync.dma_start(offsets[:], offs)
-        nc.sync.dma_start(kb_pool[ROW:P, :], kb[0:1, :])
         nc.sync.dma_start(vs_pool[ROW:P, :], vs[0:1, :])
+        nc.sync.dma_start(kb_pool[ROW:P, :], kb[0:1, :])
         nc.sync.dma_start(qw[:].bitcast(I32), q_words.rearrange("b o p q r -> p (b o) (q r)").bitcast(I32))
         ks_rows = k_scales[0].bitcast(I32).rearrange("(a r) t -> r a t", r=4)
         for r in range(4):
@@ -84,8 +88,7 @@ def tile_attend_sigm_kb_pgb2q256n512t2048_kernel(tc, q_words, q_scales, k_words,
         for b in range(B):
             nc.vector.tensor_copy(kw_d[b][:].rearrange("p t s -> p s t"), kw_pool[:].indirect(seq_list(b)))
 
-        def gather_row(pool, name, b):
-            row = sb.tile([P, N], F32, name="%s%d" % (name, b))
+        def gather_row(pool, row, b):
             nc.scalar.activation(row[:], pool[:].indirect(seq_list(b)), ACT.Copy)
             return row
 
@@ -97,8 +100,11 @@ def tile_attend_sigm_kb_pgb2q256n512t2048_kernel(tc, q_words, q_scales, k_words,
         def stepped(row):
             return [row[:, t:N:PACK] for t in range(PACK)]
 
-        kb_g = [gather_row(kb_pool, "kb_g", b) for b in reversed(range(B))]
-        vs_g = [gather_row(vs_pool, "vs_g", b) for b in range(B)]
+        vs_g = [gather_row(vs_pool, sb.tile([P, N], F32, name="vs_g0"), 0)]
+        vs_bank = [bank([P, N], "vs_bank0", 5)]
+        turn_row(vs_bank[0], stepped(vs_g[0]), 0)
+        kb_g = [gather_row(kb_pool, sb.tile([P, N], F32, name="kb_g%d" % b), b) for b in reversed(range(B))]
+        vs_g.append(gather_row(vs_pool, placed([P, N], F32, "vs_g1", kb_at), 1))
         kb_bank = bank([P, N], "kb_bank", 0)
         for n, b in enumerate(reversed(range(B))):
             turn_row(kb_bank, stepped(kb_g[n]), b * PACK)
@@ -122,9 +128,8 @@ def tile_attend_sigm_kb_pgb2q256n512t2048_kernel(tc, q_words, q_scales, k_words,
                     c = b * PACK + t
                     nc.scalar.activation(prob[b][:, t, :], score[:, u, :], ACT.Sigmoid, bias=kb_col[:, c:c + 1])
 
-        vs_bank = [bank([P, N], "vs_bank%d" % b, 1 + b) for b in range(B)]
-        for b in range(B):
-            turn_row(vs_bank[b], stepped(vs_g[b]), 0)
+        vs_bank.append(bank([P, N], "vs_bank1", 1))
+        turn_row(vs_bank[1], stepped(vs_g[1]), 0)
 
         def gather_values(h, b, on_vector):
             v_g = sb.tile([P, N], BF16, name="v_g%d%d" % (h, b), align_bytes=64)

@@ -58,10 +58,8 @@ def tile_attend_sigm_kb_pgb2q256n512t2048_kernel(tc, q_words, q_scales, k_words,
         nc.vector.memset(vs_pool[0:ROW, 0:SHARE - 1], 0.0)
         nc.vector.memset(vs_pool[0:ROW, SHARE - 1:SHARE], 0.0)
         nc.gpsimd.memset(vs_pool[0:ROW, SHARE:T], 0.0)
-        nc.vector.memset(kb_pool[0:ROW, 0:T - SHARE - 1], 0.0)
-        nc.vector.memset(kb_pool[0:ROW, T - SHARE - 1:T - SHARE], 0.0)
-        nc.gpsimd.memset(kb_pool[0:ROW, T - SHARE:T], 0.0)
         make_identity(nc, ident[:])
+        nc.vector.memset(kb_pool[0:ROW, :], 0.0)
         nc.scalar.activation(warm[:, 1:2], warm[:, 0:1], ACT.Sigmoid)
 
         nc.sync.dma_start(offsets[:], offs)

@@ -138,16 +138,18 @@ def tile_attend_sigm_kb_pgb2q256n512t2048_kernel(tc, q_words, q_scales, k_words,
                 nc.scalar.activation(v_g[:], window, ACT.Copy)
             words = v_g[:].bitcast(F32)
             for u in range(2):
-                nc.tensor.transpose(v_bank[b][:, h, u, :], words[:, u:N // 2:2], ident[:])
+                nc.tensor.transpose(v_turned[b][h][:, u, :], words[:, u:N // 2:2], ident[:])
 
-        def weave_values(b, copy):
-            v_bf = sb.tile([P, DV * PACK], BF16, name="v_bf%d" % b, align_bytes=64)
-            copy(v_bf[:].bitcast(F32).rearrange("p (h e u) -> p h e u", e=P, u=2), v_bank[b][:].rearrange("p h u e -> p h e u"))
+        def weave_values(name, turned):
+            width = turned.shape[1] * P
+            v_bf = placed([P, width * PACK], BF16, name, v0_at + T * 4) if name == "v_bf10" else sb.tile([P, width * PACK], BF16, name=name, align_bytes=64)
+            nc.scalar.copy(v_bf[:].bitcast(F32).rearrange("p (h e u) -> p h e u", e=P, u=2), turned.rearrange("p h u e -> p h e u"))
             return v_bf
 
         def quantize(name, values):
-            codes = sb.tile([P, NQ], U32, name=name + "_codes", align_bytes=64)
-            scales = sb.tile([P, NQ], U8, name=name + "_scales", align_bytes=64)
+            width = values.shape[1] // PACK
+            codes = sb.tile([P, width], U32, name=name + "_codes", align_bytes=64)
+            scales = sb.tile([P, width], U8, name=name + "_scales", align_bytes=64)
             nc.vector.quantize_mx(out=codes[:].bitcast(FP8X4), scales=scales[:], in_=values[:])
             return codes, scales
 
@@ -161,30 +163,41 @@ def tile_attend_sigm_kb_pgb2q256n512t2048_kernel(tc, q_words, q_scales, k_words,
             )
             return w_bf
 
-        def finish(b, m, w_q, v_q, n, on_vector):
-            acc = bank([P, DV], "acc%d%d" % (b, m), n)
+        def multiply(acc, m, w_q, v_q):
             rows = slice(m * P, (m + 1) * P)
             nc.tensor.matmul_mx(
-                out=acc[:],
+                out=acc,
                 lhsT=w_q[0][:, rows].bitcast(FP8X4), lhsT_scale=w_q[1][:, rows],
                 rhs=v_q[0][:].bitcast(FP8X4), rhs_scale=v_q[1][:],
                 start=True, stop=True,
             )
+
+        def finish(b, m, acc, on_vector):
             y = sb.tile([P, DV], F32, name="y%d%d" % (b, m))
             if on_vector:
                 nc.vector.tensor_scalar(y[:], acc[:], 1.0 / 16.0, None, ALU.mult)
             else:
                 nc.scalar.activation(y[:], acc[:], ACT.Copy, scale=1.0 / 16.0)
-            nc.sync.dma_start(out[b, rows, :], y[:])
+            nc.sync.dma_start(out[b, m * P:(m + 1) * P, :], y[:])
 
-        v_bank = [bank([P, HALVES, 2, P], "v_bank%d" % b, 3 + b) for b in range(B)]
+        v_bank0 = bank([P, HALVES, 2, P], "v_bank0", 3)
+        v_bank1 = [bank([P, 1, 2, P], "v_bank1%d" % h, (4, 2)[h]) for h in range(HALVES)]
+        v_turned = [[v_bank0[:, h] for h in range(HALVES)], [v_bank1[h][:, 0] for h in range(HALVES)]]
         for h in range(HALVES):
             for b in range(B):
                 gather_values(h, b, h == 0)
         w_bf = [weigh(b) for b in range(B)]
         w_q = [quantize("w%d" % b, w_bf[b]) for b in range(B)]
-        v_bf = [weave_values(b, nc.scalar.copy) for b in range(B)]
-        v_q = [quantize("v%d" % b, v_bf[b]) for b in range(B)]
-        for b in range(B):
+        v_bf0 = weave_values("v_bf0", v_bank0[:])
+        v_bf1 = [weave_values("v_bf1%d" % h, v_bank1[h][:]) for h in range(HALVES)]
+        v_q0 = quantize("v0", v_bf0)
+        v_q1 = [quantize("v1%d" % h, v_bf1[h]) for h in range(HALVES)]
+        acc = [[bank([P, DV], "acc%d%d" % (b, m), (5, 6, 7, 0)[2 * b + m]) for m in range(2)] for b in range(B)]
+        for m in range(2):
+            multiply(acc[0][m][:], m, w_q[0], v_q0)
+            finish(0, m, acc[0][m], False)
+        for h in range(HALVES):
             for m in range(2):
-                finish(b, m, w_q[b], v_q[b], (5, 6, 7, 0)[2 * b + m], (b, m) == (1, 0))
+                multiply(acc[1][m][:, h * P:(h + 1) * P], m, w_q[1], v_q1[h])
+        for m in range(2):
+            finish(1, m, acc[1][m], m == 0)

@@ -23,6 +23,7 @@ HALVES = DV // P
 LIST_COLS = N // 16
 TURN_STEP = 8
 SHARE = T * 3 // 4
+KEYS_FIRST = T * 3 // 8
 
 
 def tile_attend_sigm_kb_pgb2q256n512t2048_kernel(tc, q_words, q_scales, k_words, k_scales, vT, vs, kb, offs, out):
@@ -65,11 +66,13 @@ def tile_attend_sigm_kb_pgb2q256n512t2048_kernel(tc, q_words, q_scales, k_words,
         nc.sync.dma_start(offsets[:], offs)
         nc.sync.dma_start(vs_pool[ROW:P, :], vs[0:1, :])
         nc.sync.dma_start(kb_pool[ROW:P, :], kb[0:1, :])
-        nc.sync.dma_start(qw[:].bitcast(I32), q_words.rearrange("b o p q r -> p (b o) (q r)").bitcast(I32))
+        key_words = k_words[0].rearrange("p t r -> p (t r)").bitcast(I32)
+        nc.sync.dma_start(kw_pool[:].bitcast(I32)[:, 0:KEYS_FIRST], key_words[:, 0:KEYS_FIRST])
         ks_rows = k_scales[0].bitcast(I32).rearrange("(a r) t -> r a t", r=4)
         for r in range(4):
             nc.sync.dma_start(ks_pool[:].bitcast(I32)[r:P:32, :], ks_rows[r])
-        nc.sync.dma_start(kw_pool[:].bitcast(I32), k_words[0].rearrange("p t r -> p (t r)").bitcast(I32))
+        nc.sync.dma_start(kw_pool[:].bitcast(I32)[:, KEYS_FIRST:T], key_words[:, KEYS_FIRST:T])
+        nc.sync.dma_start(qw[:].bitcast(I32), q_words.rearrange("b o p q r -> p (b o) (q r)").bitcast(I32))
         qs_rows = q_scales.bitcast(I32).rearrange("b o (a r) q -> r a (b o) q", r=4)
         for r in range(4):
             nc.sync.dma_start(qs[:].bitcast(I32)[r:P:32, :, :], qs_rows[r])

@@ -23,7 +23,7 @@ HALVES = DV // P
 LIST_COLS = N // 16
 TURN_STEP = 8
 SHARE = T * 3 // 4
-KEYS_FIRST = T * 3 // 8
+KEYS_FIRST = T * 3 // 16
 
 
 def tile_attend_sigm_kb_pgb2q256n512t2048_kernel(tc, q_words, q_scales, k_words, k_scales, vT, vs, kb, offs, out):
@@ -65,9 +65,9 @@ def tile_attend_sigm_kb_pgb2q256n512t2048_kernel(tc, q_words, q_scales, k_words,
 
         nc.sync.dma_start(offsets[:], offs)
         nc.sync.dma_start(vs_pool[ROW:P, :], vs[0:1, :])
-        nc.sync.dma_start(kb_pool[ROW:P, :], kb[0:1, :])
         key_words = k_words[0].rearrange("p t r -> p (t r)").bitcast(I32)
         nc.sync.dma_start(kw_pool[:].bitcast(I32)[:, 0:KEYS_FIRST], key_words[:, 0:KEYS_FIRST])
+        nc.sync.dma_start(kb_pool[ROW:P, :], kb[0:1, :])
         ks_rows = k_scales[0].bitcast(I32).rearrange("(a r) t -> r a t", r=4)
         for r in range(4):
             nc.sync.dma_start(ks_pool[:].bitcast(I32)[r:P:32, :], ks_rows[r])
@@ -175,13 +175,11 @@ def tile_attend_sigm_kb_pgb2q256n512t2048_kernel(tc, q_words, q_scales, k_words,
                 start=True, stop=True,
             )
 
-        def finish(b, m, acc, on_vector):
-            y = sb.tile([P, DV], F32, name="y%d%d" % (b, m))
+        def scale_out(y, acc, on_vector):
             if on_vector:
-                nc.vector.tensor_scalar(y[:], acc[:], 1.0 / 16.0, None, ALU.mult)
+                nc.vector.tensor_scalar(y, acc, 1.0 / 16.0, None, ALU.mult)
             else:
-                nc.scalar.activation(y[:], acc[:], ACT.Copy, scale=1.0 / 16.0)
-            nc.sync.dma_start(out[b, m * P:(m + 1) * P, :], y[:])
+                nc.scalar.activation(y, acc, ACT.Copy, scale=1.0 / 16.0)
 
         v_bank0 = bank([P, HALVES, 2, P], "v_bank0", 3)
         v_bank1 = [bank([P, 1, 2, P], "v_bank1%d" % h, (4, 2)[h]) for h in range(HALVES)]
@@ -195,12 +193,16 @@ def tile_attend_sigm_kb_pgb2q256n512t2048_kernel(tc, q_words, q_scales, k_words,
         v_bf1 = [weave_values("v_bf1%d" % h, v_bank1[h][:]) for h in range(HALVES)]
         v_q0 = quantize("v0", v_bf0)
         v_q1 = [quantize("v1%d" % h, v_bf1[h]) for h in range(HALVES)]
-        acc = [[bank([P, DV], "acc%d%d" % (b, m), (5, 6, 7, 0)[2 * b + m]) for m in range(2)] for b in range(B)]
+        y = [[sb.tile([P, DV], F32, name="y%d%d" % (b, m)) for m in range(2)] for b in range(B)]
         for m in range(2):
-            multiply(acc[0][m][:], m, w_q[0], v_q0)
-            finish(0, m, acc[0][m], False)
+            acc = bank([P, DV], "acc0%d" % m, 5 + m)
+            multiply(acc[:], m, w_q[0], v_q0)
+            scale_out(y[0][m][:], acc[:], m == 1)
+            nc.sync.dma_start(out[0, m * P:(m + 1) * P, :], y[0][m][:])
         for h in range(HALVES):
             for m in range(2):
-                multiply(acc[1][m][:, h * P:(h + 1) * P], m, w_q[1], v_q1[h])
+                acc = bank([P, P], "acc1%d%d" % (m, h), (7, 0, 1, 3)[2 * h + m])
+                multiply(acc[:], m, w_q[1], v_q1[h])
+                scale_out(y[1][m][:, h * P:(h + 1) * P], acc[:], m == 0)
         for m in range(2):
-            finish(1, m, acc[1][m], m == 0)
+            nc.sync.dma_start(out[1, m * P:(m + 1) * P, :], y[1][m][:])

@@ -41,10 +41,9 @@ def tile_attend_sigm_kb_pgb2q256n512t2048_kernel(tc, q_words, q_scales, k_words,
 
         vs_at = 0
         v0_at = vs_at + T * 4
-        kb_at = v0_at + HALVES * T * 4
 
         offsets = sb.tile([P, B * LIST_COLS], U16, name="offsets")
-        kb_pool = placed([P, T], F32, "kb_pool", kb_at)
+        kb_pool = sb.tile([P, T], F32, name="kb_pool")
         vs_pool = placed([P, T], F32, "vs_pool", vs_at)
         ks_pool = sb.tile([P, T], U8, name="ks_pool")
         kw_pool = sb.tile([P, T], U32, name="kw_pool")
@@ -56,18 +55,18 @@ def tile_attend_sigm_kb_pgb2q256n512t2048_kernel(tc, q_words, q_scales, k_words,
         nc.gpsimd.memset(ks_pool[:].bitcast(I32), 0)
         nc.vector.memset(qs[:].rearrange("p b q -> p (b q)").bitcast(I32), 0)
         nc.vector.memset(warm[:, 0:1], 0.0)
-        nc.vector.memset(vs_pool[0:ROW, 0:SHARE - 1], 0.0)
-        nc.vector.memset(vs_pool[0:ROW, SHARE - 1:SHARE], 0.0)
-        nc.gpsimd.memset(vs_pool[0:ROW, SHARE:T], 0.0)
+        nc.vector.memset(kb_pool[0:ROW, 0:SHARE - 1], 0.0)
+        nc.vector.memset(kb_pool[0:ROW, SHARE - 1:SHARE], 0.0)
+        nc.gpsimd.memset(kb_pool[0:ROW, SHARE:T], 0.0)
         make_identity(nc, ident[:])
-        nc.vector.memset(kb_pool[0:ROW, :], 0.0)
+        nc.vector.memset(vs_pool[0:ROW, :], 0.0)
         nc.scalar.activation(warm[:, 1:2], warm[:, 0:1], ACT.Sigmoid)
 
         nc.sync.dma_start(offsets[:], offs)
-        nc.sync.dma_start(vs_pool[ROW:P, :], vs[0:1, :])
+        nc.sync.dma_start(kb_pool[ROW:P, :], kb[0:1, :])
         key_words = k_words[0].rearrange("p t r -> p (t r)").bitcast(I32)
         nc.sync.dma_start(kw_pool[:].bitcast(I32)[:, 0:KEYS_FIRST], key_words[:, 0:KEYS_FIRST])
-        nc.sync.dma_start(kb_pool[ROW:P, :], kb[0:1, :])
+        nc.sync.dma_start(vs_pool[ROW:P, :], vs[0:1, :])
         ks_rows = k_scales[0].bitcast(I32).rearrange("(a r) t -> r a t", r=4)
         for r in range(4):
             nc.sync.dma_start(ks_pool[:].bitcast(I32)[r:P:32, :], ks_rows[r])
@@ -89,48 +88,42 @@ def tile_attend_sigm_kb_pgb2q256n512t2048_kernel(tc, q_words, q_scales, k_words,
         for b in range(B):
             nc.vector.tensor_copy(kw_d[b][:].rearrange("p t s -> p s t"), kw_pool[:].indirect(seq_list(b)))
 
-        def gather_row(pool, row, b):
+        def gather_row(pool, name, b):
+            row = sb.tile([P, N], F32, name="%s%d" % (name, b))
             nc.scalar.activation(row[:], pool[:].indirect(seq_list(b)), ACT.Copy)
             return row
 
-        def turn_row(dst, places, first):
+        def turn_row(dst, row, first):
             for t in reversed(range(PACK)):
                 at = (first + t) * TURN_STEP
-                nc.tensor.transpose(dst[:, at:at + P], places[t], ident[:])
+                nc.tensor.transpose(dst[:, at:at + P], row[:, t:N:PACK], ident[:])
 
-        def stepped(row):
-            return [row[:, t:N:PACK] for t in range(PACK)]
-
-        vs_g = [gather_row(vs_pool, sb.tile([P, N], F32, name="vs_g0"), 0)]
-        vs_bank = [bank([P, N], "vs_bank0", 5)]
-        turn_row(vs_bank[0], stepped(vs_g[0]), 0)
-        kb_g = [gather_row(kb_pool, sb.tile([P, N], F32, name="kb_g%d" % b), b) for b in reversed(range(B))]
-        vs_g.append(gather_row(vs_pool, placed([P, N], F32, "vs_g1", kb_at), 1))
+        kb_g = [gather_row(kb_pool, "kb_g", b) for b in reversed(range(B))]
+        vs_g = [gather_row(vs_pool, "vs_g", b) for b in range(B)]
         kb_bank = bank([P, N], "kb_bank", 0)
         for n, b in enumerate(reversed(range(B))):
-            turn_row(kb_bank, stepped(kb_g[n]), b * PACK)
+            turn_row(kb_bank, kb_g[n], b * PACK)
         kb_col = placed([P, B * PACK], F32, "kb_col", vs_at)
         nc.scalar.copy(kb_col[:], kb_bank[:, ROW:ROW + B * PACK * TURN_STEP:TURN_STEP])
 
         prob = [sb.tile([P, PACK, NQ], F32, name="prob%d" % b, align_bytes=64) for b in range(B)]
-        for b in range(B):
-            for half in range(2):
-                score = bank([P, 2, NQ], "score%d%d" % (b, half), 1 + 2 * b + half)
-                for u in range(2):
-                    t = 2 * half + u
-                    nc.tensor.matmul_mx(
-                        out=score[:, u, :],
-                        lhsT=kw_d[b][:, t, :].bitcast(FP8X4), lhsT_scale=ks_d[:, b, t, :],
-                        rhs=qw[:, b, :].bitcast(FP8X4), rhs_scale=qs[:, b, :],
-                        start=True, stop=True,
-                    )
-                for u in range(2):
-                    t = 2 * half + u
-                    c = b * PACK + t
-                    nc.scalar.activation(prob[b][:, t, :], score[:, u, :], ACT.Sigmoid, bias=kb_col[:, c:c + 1])
+        score_groups = [(0, (0,)), (0, (1,)), (0, (2, 3)), (1, (0, 1)), (1, (2, 3))]
+        for n, (b, places) in enumerate(score_groups):
+            score = bank([P, len(places), NQ], "score%d" % n, 1 + n)
+            for u, t in enumerate(places):
+                nc.tensor.matmul_mx(
+                    out=score[:, u, :],
+                    lhsT=kw_d[b][:, t, :].bitcast(FP8X4), lhsT_scale=ks_d[:, b, t, :],
+                    rhs=qw[:, b, :].bitcast(FP8X4), rhs_scale=qs[:, b, :],
+                    start=True, stop=True,
+                )
+            for u, t in enumerate(places):
+                c = b * PACK + t
+                nc.scalar.activation(prob[b][:, t, :], score[:, u, :], ACT.Sigmoid, bias=kb_col[:, c:c + 1])
 
-        vs_bank.append(bank([P, N], "vs_bank1", 1))
-        turn_row(vs_bank[1], stepped(vs_g[1]), 0)
+        vs_bank = [bank([P, N], "vs_bank%d" % b, 2 + b) for b in range(B)]
+        for b in range(B):
+            turn_row(vs_bank[b], vs_g[b], 0)
 
         def gather_values(h, b, on_vector):
             v_g = sb.tile([P, N], BF16, name="v_g%d%d" % (h, b), align_bytes=64)
@@ -181,8 +174,8 @@ def tile_attend_sigm_kb_pgb2q256n512t2048_kernel(tc, q_words, q_scales, k_words,
             else:
                 nc.scalar.activation(y, acc, ACT.Copy, scale=1.0 / 16.0)
 
-        v_bank0 = bank([P, HALVES, 2, P], "v_bank0", 3)
-        v_bank1 = [bank([P, 1, 2, P], "v_bank1%d" % h, (4, 2)[h]) for h in range(HALVES)]
+        v_bank0 = bank([P, HALVES, 2, P], "v_bank0", 4)
+        v_bank1 = [bank([P, 1, 2, P], "v_bank1%d" % h, (5, 1)[h]) for h in range(HALVES)]
         v_turned = [[v_bank0[:, h] for h in range(HALVES)], [v_bank1[h][:, 0] for h in range(HALVES)]]
         for h in range(HALVES):
             for b in range(B):
@@ -195,13 +188,13 @@ def tile_attend_sigm_kb_pgb2q256n512t2048_kernel(tc, q_words, q_scales, k_words,
         v_q1 = [quantize("v1%d" % h, v_bf1[h]) for h in range(HALVES)]
         y = [[sb.tile([P, DV], F32, name="y%d%d" % (b, m)) for m in range(2)] for b in range(B)]
         for m in range(2):
-            acc = bank([P, DV], "acc0%d" % m, 5 + m)
+            acc = bank([P, DV], "acc0%d" % m, 6 + m)
             multiply(acc[:], m, w_q[0], v_q0)
             scale_out(y[0][m][:], acc[:], m == 1)
             nc.sync.dma_start(out[0, m * P:(m + 1) * P, :], y[0][m][:])
         for h in range(HALVES):
             for m in range(2):
-                acc = bank([P, P], "acc1%d%d" % (m, h), (7, 0, 1, 3)[2 * h + m])
+                acc = bank([P, P], "acc1%d%d" % (m, h), (0, 2, 3, 4)[2 * h + m])
                 multiply(acc[:], m, w_q[1], v_q1[h])
                 scale_out(y[1][m][:, h * P:(h + 1) * P], acc[:], m == 0)
         for m in range(2):

@@ -22,7 +22,9 @@ ROW = P - 1
 HALVES = DV // P
 LIST_COLS = N // 16
 TURN_STEP = 8
-SHARE = T * 3 // 4
+KB_SHARE = T * 3 // 4
+VS_SHARE = T // 4
+BIAS_SHARE = 256
 KEYS_FIRST = T * 3 // 16
 
 
@@ -40,7 +42,8 @@ def tile_attend_sigm_kb_pgb2q256n512t2048_kernel(tc, q_words, q_scales, k_words,
             return ps.tile(shape, F32, name=name, tag="bank%d" % n)
 
         vs_at = 0
-        v0_at = vs_at + T * 4
+        v1_at = vs_at + T * 4
+        v0_at = v1_at + T * 4
 
         offsets = sb.tile([P, B * LIST_COLS], U16, name="offsets")
         kb_pool = sb.tile([P, T], F32, name="kb_pool")
@@ -52,15 +55,19 @@ def tile_attend_sigm_kb_pgb2q256n512t2048_kernel(tc, q_words, q_scales, k_words,
         qw = sb.tile([P, B, NQ], U32, name="qw", align_bytes=64)
         warm = sb.tile([P, 2], F32, name="warm")
 
-        nc.gpsimd.memset(ks_pool[:].bitcast(I32), 0)
+        def zero_on_vector(tile, rows, first, last):
+            nc.vector.memset(tile[0:rows, first:last - 1], 0)
+            nc.vector.memset(tile[0:rows, last - 1:last], 0)
+
         nc.vector.memset(qs[:].rearrange("p b q -> p (b q)").bitcast(I32), 0)
         nc.vector.memset(warm[:, 0:1], 0.0)
-        nc.vector.memset(kb_pool[0:ROW, 0:SHARE - 1], 0.0)
-        nc.vector.memset(kb_pool[0:ROW, SHARE - 1:SHARE], 0.0)
-        nc.gpsimd.memset(kb_pool[0:ROW, SHARE:T], 0.0)
-        make_identity(nc, ident[:])
-        nc.vector.memset(vs_pool[0:ROW, :], 0.0)
         nc.scalar.activation(warm[:, 1:2], warm[:, 0:1], ACT.Sigmoid)
+        nc.gpsimd.memset(ks_pool[:].bitcast(I32), 0)
+        zero_on_vector(kb_pool, ROW, 0, KB_SHARE)
+        nc.gpsimd.memset(kb_pool[0:ROW, KB_SHARE:T], 0.0)
+        zero_on_vector(vs_pool, ROW, 0, VS_SHARE)
+        make_identity(nc, ident[:])
+        nc.gpsimd.memset(vs_pool[0:ROW, VS_SHARE:T], 0.0)
 
         nc.sync.dma_start(offsets[:], offs)
         nc.sync.dma_start(kb_pool[ROW:P, :], kb[0:1, :])
@@ -75,83 +82,79 @@ def tile_attend_sigm_kb_pgb2q256n512t2048_kernel(tc, q_words, q_scales, k_words,
         qs_rows = q_scales.bitcast(I32).rearrange("b o (a r) q -> r a (b o) q", r=4)
         for r in range(4):
             nc.sync.dma_start(qs[:].bitcast(I32)[r:P:32, :, :], qs_rows[r])
-        v_pool = [placed([P, T], F32, "v_pool%d" % h, v0_at + h * T * 4) for h in range(HALVES)]
+        v_pool = [placed([P, T], F32, "v_pool0", v0_at), placed([P, T], F32, "v_pool1", v1_at)]
         for h in range(HALVES):
             nc.sync.dma_start(v_pool[h][:], vT[h * P:(h + 1) * P, :])
 
-        def seq_list(b):
-            return offsets[:, b * LIST_COLS:(b + 1) * LIST_COLS]
+        def entries(b, first=0, last=N):
+            return offsets[:, b * LIST_COLS + first // 16:b * LIST_COLS + last // 16]
 
-        ks_d = sb.tile([P, B, PACK, P], U8, name="ks_d", align_bytes=64)
-        nc.vector.tensor_copy(ks_d[:].rearrange("p b t s -> p b s t"), ks_pool[:].indirect(offsets[:]))
-        kw_d = [sb.tile([P, PACK, P], U32, name="kw_d%d" % b, align_bytes=64) for b in range(B)]
-        for b in range(B):
-            nc.vector.tensor_copy(kw_d[b][:].rearrange("p t s -> p s t"), kw_pool[:].indirect(seq_list(b)))
+        def deal(dst, pool, b):
+            nc.vector.tensor_copy(dst[:].rearrange("p t s -> p s t"), pool[:].indirect(entries(b)))
 
-        def gather_row(pool, name, b):
+        def gather_row(pool, name, b, on_vector=0):
             row = sb.tile([P, N], F32, name="%s%d" % (name, b))
-            nc.scalar.activation(row[:], pool[:].indirect(seq_list(b)), ACT.Copy)
-            return row
+            if on_vector:
+                nc.vector.tensor_copy(row[:, 0:on_vector], pool[:].indirect(entries(b, 0, on_vector)))
+            nc.scalar.activation(row[:, on_vector:N], pool[:].indirect(entries(b, on_vector, N)), ACT.Copy)
+            return row[:].rearrange("p (s t) -> p t s", t=PACK)
 
         def turn_row(dst, row, first):
             for t in reversed(range(PACK)):
                 at = (first + t) * TURN_STEP
-                nc.tensor.transpose(dst[:, at:at + P], row[:, t:N:PACK], ident[:])
+                nc.tensor.transpose(dst[:, at:at + P], row[:, t, :], ident[:])
 
-        kb_g = [gather_row(kb_pool, "kb_g", b) for b in reversed(range(B))]
+        kb_g = [gather_row(kb_pool, "kb_g", 1, BIAS_SHARE), gather_row(kb_pool, "kb_g", 0)]
         vs_g = [gather_row(vs_pool, "vs_g", b) for b in range(B)]
         kb_bank = bank([P, N], "kb_bank", 0)
         for n, b in enumerate(reversed(range(B))):
             turn_row(kb_bank, kb_g[n], b * PACK)
         kb_col = placed([P, B * PACK], F32, "kb_col", vs_at)
         nc.scalar.copy(kb_col[:], kb_bank[:, ROW:ROW + B * PACK * TURN_STEP:TURN_STEP])
+        vs_bank0 = bank([P, N], "vs_bank0", 6)
+        turn_row(vs_bank0, vs_g[0], 0)
 
+        kw_d = [sb.tile([P, PACK, P], U32, name="kw_d0", align_bytes=64), sb.tile([P, PACK, P], U32, name="kw_d1", align_bytes=64)]
         prob = [sb.tile([P, PACK, NQ], F32, name="prob%d" % b, align_bytes=64) for b in range(B)]
-        score_groups = [(0, (0,)), (0, (1,)), (0, (2, 3)), (1, (0, 1)), (1, (2, 3))]
-        for n, (b, places) in enumerate(score_groups):
-            score = bank([P, len(places), NQ], "score%d" % n, 1 + n)
-            for u, t in enumerate(places):
-                nc.tensor.matmul_mx(
-                    out=score[:, u, :],
-                    lhsT=kw_d[b][:, t, :].bitcast(FP8X4), lhsT_scale=ks_d[:, b, t, :],
-                    rhs=qw[:, b, :].bitcast(FP8X4), rhs_scale=qs[:, b, :],
-                    start=True, stop=True,
-                )
-            for u, t in enumerate(places):
-                c = b * PACK + t
-                nc.scalar.activation(prob[b][:, t, :], score[:, u, :], ACT.Sigmoid, bias=kb_col[:, c:c + 1])
 
-        vs_bank = [bank([P, N], "vs_bank%d" % b, 2 + b) for b in range(B)]
-        for b in range(B):
-            turn_row(vs_bank[b], vs_g[b], 0)
+        def scores(b, groups):
+            for n, places in groups:
+                score = bank([P, len(places), NQ], "score%d%d" % (b, places[0]), n)
+                for u, t in enumerate(places):
+                    nc.tensor.matmul_mx(
+                        out=score[:, u, :],
+                        lhsT=kw_d[b][:, t, :].bitcast(FP8X4), lhsT_scale=ks_d[:, b, t, :],
+                        rhs=qw[:, b, :].bitcast(FP8X4), rhs_scale=qs[:, b, :],
+                        start=True, stop=True,
+                    )
+                for u, t in enumerate(places):
+                    nc.scalar.activation(prob[b][:, t, :], score[:, u, :], ACT.Sigmoid, bias=kb_col[:, b * PACK + t:b * PACK + t + 1])
 
-        def gather_values(h, b, on_vector):
-            v_g = sb.tile([P, N], BF16, name="v_g%d%d" % (h, b), align_bytes=64)
-            window = v_pool[h][:].indirect(seq_list(b))
+        def gather_values(v_g, h, b, on_vector):
+            window = v_pool[h][:].indirect(entries(b))
             if on_vector:
                 nc.vector.tensor_copy(v_g[:], window)
             else:
                 nc.scalar.activation(v_g[:], window, ACT.Copy)
+
+        def turn_values(dst, v_g):
             words = v_g[:].bitcast(F32)
             for u in range(2):
-                nc.tensor.transpose(v_turned[b][h][:, u, :], words[:, u:N // 2:2], ident[:])
+                nc.tensor.transpose(dst[:, u, :], words[:, u:N // 2:2], ident[:])
 
-        def weave_values(name, turned):
-            width = turned.shape[1] * P
-            v_bf = placed([P, width * PACK], BF16, name, v0_at + T * 4) if name == "v_bf10" else sb.tile([P, width * PACK], BF16, name=name, align_bytes=64)
+        def weave_values(v_bf, turned):
             nc.scalar.copy(v_bf[:].bitcast(F32).rearrange("p (h e u) -> p h e u", e=P, u=2), turned.rearrange("p h u e -> p h e u"))
-            return v_bf
 
-        def quantize(name, values):
-            width = values.shape[1] // PACK
-            codes = sb.tile([P, width], U32, name=name + "_codes", align_bytes=64)
-            scales = sb.tile([P, width], U8, name=name + "_scales", align_bytes=64)
+        def quantize(values, codes, scales):
             nc.vector.quantize_mx(out=codes[:].bitcast(FP8X4), scales=scales[:], in_=values[:])
             return codes, scales
 
-        def weigh(b):
-            w_bf = placed([P, NQ * PACK], BF16, "w_bf%d" % b, v0_at + b * NQ * PACK * 2)
-            scale = vs_bank[b][:, ROW:ROW + PACK * TURN_STEP:TURN_STEP].unsqueeze(1).unsqueeze(3).to_broadcast([P, NQ // 4, PACK, 4])
+        def planes(name, width):
+            return (sb.tile([P, width], U32, name=name + "_codes", align_bytes=64),
+                    sb.tile([P, width], U8, name=name + "_scales", align_bytes=64))
+
+        def weigh(b, vs_bank, w_bf):
+            scale = vs_bank[:, ROW:ROW + PACK * TURN_STEP:TURN_STEP].unsqueeze(1).unsqueeze(3).to_broadcast([P, NQ // 4, PACK, 4])
             nc.vector.tensor_tensor(
                 w_bf[:].rearrange("p (c i t) -> p c t i", i=4, t=PACK),
                 prob[b][:].rearrange("p t (c i) -> p c t i", i=4),
@@ -174,27 +177,48 @@ def tile_attend_sigm_kb_pgb2q256n512t2048_kernel(tc, q_words, q_scales, k_words,
             else:
                 nc.scalar.activation(y, acc, ACT.Copy, scale=1.0 / 16.0)
 
-        v_bank0 = bank([P, HALVES, 2, P], "v_bank0", 4)
-        v_bank1 = [bank([P, 1, 2, P], "v_bank1%d" % h, (5, 1)[h]) for h in range(HALVES)]
-        v_turned = [[v_bank0[:, h] for h in range(HALVES)], [v_bank1[h][:, 0] for h in range(HALVES)]]
+        v_g = [[sb.tile([P, N], BF16, name="v_g%d%d" % (h, b), align_bytes=64) for b in range(B)] for h in range(HALVES)]
+
+        ks_d = sb.tile([P, B, PACK, P], U8, name="ks_d", align_bytes=64)
+        nc.vector.tensor_copy(ks_d[:].rearrange("p b t s -> p b s t"), ks_pool[:].indirect(offsets[:]))
+        for b in range(B):
+            deal(kw_d[b], kw_pool, b)
+        scores(0, [(1, (0,)), (2, (1,)), (3, (2, 3))])
+        scores(1, [(4, (0, 1)), (5, (2, 3))])
+        vs_bank1 = bank([P, N], "vs_bank1", 1)
+        turn_row(vs_bank1, vs_g[1], 0)
+        gather_values(v_g[0][0], 0, 0, True)
+        gather_values(v_g[0][1], 0, 1, True)
+        w_bf0 = weigh(0, vs_bank0, placed([P, NQ * PACK], BF16, "w_bf0", v0_at))
+
+        v_bank0 = bank([P, HALVES, 2, P], "v_bank0", 7)
+        v_bank1 = [bank([P, 1, 2, P], "v_bank1%d" % h, (2, 0)[h]) for h in range(HALVES)]
+        turn_values(v_bank0[:, 0], v_g[0][0])
+        turn_values(v_bank1[0][:, 0], v_g[0][1])
+        gather_values(v_g[1][0], 1, 0, False)
+        turn_values(v_bank0[:, 1], v_g[1][0])
+        gather_values(v_g[1][1], 1, 1, False)
+        turn_values(v_bank1[1][:, 0], v_g[1][1])
+        w_bf1 = weigh(1, vs_bank1, placed([P, NQ * PACK], BF16, "w_bf1", v0_at + NQ * PACK * 2))
+        w_q = [quantize(w_bf0, *planes("w0", NQ)), quantize(w_bf1, *planes("w1", NQ))]
+
+        v_bf0 = sb.tile([P, DV * PACK], BF16, name="v_bf0", align_bytes=64)
+        weave_values(v_bf0, v_bank0[:])
+        v_bf1 = [placed([P, P * PACK], BF16, "v_bf10", v1_at), sb.tile([P, P * PACK], BF16, name="v_bf11", align_bytes=64)]
         for h in range(HALVES):
-            for b in range(B):
-                gather_values(h, b, h == 0)
-        w_bf = [weigh(b) for b in range(B)]
-        w_q = [quantize("w%d" % b, w_bf[b]) for b in range(B)]
-        v_bf0 = weave_values("v_bf0", v_bank0[:])
-        v_bf1 = [weave_values("v_bf1%d" % h, v_bank1[h][:]) for h in range(HALVES)]
-        v_q0 = quantize("v0", v_bf0)
-        v_q1 = [quantize("v1%d" % h, v_bf1[h]) for h in range(HALVES)]
+            weave_values(v_bf1[h], v_bank1[h][:])
+        v_q0 = quantize(v_bf0, *planes("v0", DV))
+        v_q1 = [quantize(v_bf1[h], *planes("v1%d" % h, P)) for h in range(HALVES)]
+
         y = [[sb.tile([P, DV], F32, name="y%d%d" % (b, m)) for m in range(2)] for b in range(B)]
         for m in range(2):
-            acc = bank([P, DV], "acc0%d" % m, 6 + m)
+            acc = bank([P, DV], "acc0%d" % m, (3, 4)[m])
             multiply(acc[:], m, w_q[0], v_q0)
             scale_out(y[0][m][:], acc[:], m == 1)
             nc.sync.dma_start(out[0, m * P:(m + 1) * P, :], y[0][m][:])
         for h in range(HALVES):
             for m in range(2):
-                acc = bank([P, P], "acc1%d%d" % (m, h), (0, 2, 3, 4)[2 * h + m])
+                acc = bank([P, P], "acc1%d%d" % (m, h), (5, 6, 1, 2)[2 * h + m])
                 multiply(acc[:], m, w_q[1], v_q1[h])
                 scale_out(y[1][m][:, h * P:(h + 1) * P], acc[:], m == 0)
         for m in range(2):

@@ -106,13 +106,14 @@ def tile_attend_sigm_kb_pgb2q256n512t2048_kernel(tc, q_words, q_scales, k_words,
 
         kb_g = [gather_row(kb_pool, "kb_g", 1, BIAS_SHARE), gather_row(kb_pool, "kb_g", 0)]
         vs_g = [gather_row(vs_pool, "vs_g", b) for b in range(B)]
+        vs_d = [sb.tile([P, PACK, P], F32, name="vs_d%d" % b) for b in range(B)]
+        for b in range(B):
+            nc.scalar.copy(vs_d[b][:].rearrange("p t s -> p s t"), vs_g[b].rearrange("p t s -> p s t"))
         kb_bank = bank([P, N], "kb_bank", 0)
         for n, b in enumerate(reversed(range(B))):
             turn_row(kb_bank, kb_g[n], b * PACK)
         kb_col = placed([P, B * PACK], F32, "kb_col", vs_at)
         nc.scalar.copy(kb_col[:], kb_bank[:, ROW:ROW + B * PACK * TURN_STEP:TURN_STEP])
-        vs_bank0 = bank([P, N], "vs_bank0", 6)
-        turn_row(vs_bank0, vs_g[0], 0)
 
         kw_d = [sb.tile([P, PACK, P], U32, name="kw_d0", align_bytes=64), sb.tile([P, PACK, P], U32, name="kw_d1", align_bytes=64)]
         prob = [sb.tile([P, PACK, NQ], F32, name="prob%d" % b, align_bytes=64) for b in range(B)]
@@ -185,21 +186,22 @@ def tile_attend_sigm_kb_pgb2q256n512t2048_kernel(tc, q_words, q_scales, k_words,
             deal(kw_d[b], kw_pool, b)
         scores(0, [(1, (0,)), (2, (1,)), (3, (2, 3))])
         scores(1, [(4, (0, 1)), (5, (2, 3))])
-        vs_bank1 = bank([P, N], "vs_bank1", 1)
-        turn_row(vs_bank1, vs_g[1], 0)
+        vs_bank = [bank([P, N], "vs_bank%d" % b, 1 + b) for b in range(B)]
+        for b in range(B):
+            turn_row(vs_bank[b], vs_d[b][:], 0)
         gather_values(v_g[0][0], 0, 0, True)
         gather_values(v_g[0][1], 0, 1, True)
-        w_bf0 = weigh(0, vs_bank0, placed([P, NQ * PACK], BF16, "w_bf0", v0_at))
+        w_bf0 = weigh(0, vs_bank[0], placed([P, NQ * PACK], BF16, "w_bf0", v0_at))
 
         v_bank0 = bank([P, HALVES, 2, P], "v_bank0", 7)
-        v_bank1 = [bank([P, 1, 2, P], "v_bank1%d" % h, (2, 0)[h]) for h in range(HALVES)]
+        v_bank1 = [bank([P, 1, 2, P], "v_bank1%d" % h, (6, 0)[h]) for h in range(HALVES)]
         turn_values(v_bank0[:, 0], v_g[0][0])
         turn_values(v_bank1[0][:, 0], v_g[0][1])
         gather_values(v_g[1][0], 1, 0, False)
         turn_values(v_bank0[:, 1], v_g[1][0])
         gather_values(v_g[1][1], 1, 1, False)
         turn_values(v_bank1[1][:, 0], v_g[1][1])
-        w_bf1 = weigh(1, vs_bank1, placed([P, NQ * PACK], BF16, "w_bf1", v0_at + NQ * PACK * 2))
+        w_bf1 = weigh(1, vs_bank[1], placed([P, NQ * PACK], BF16, "w_bf1", v0_at + NQ * PACK * 2))
         w_q = [quantize(w_bf0, *planes("w0", NQ)), quantize(w_bf1, *planes("w1", NQ))]
 
         v_bf0 = sb.tile([P, DV * PACK], BF16, name="v_bf0", align_bytes=64)
@@ -218,7 +220,7 @@ def tile_attend_sigm_kb_pgb2q256n512t2048_kernel(tc, q_words, q_scales, k_words,
             nc.sync.dma_start(out[0, m * P:(m + 1) * P, :], y[0][m][:])
         for h in range(HALVES):
             for m in range(2):
-                acc = bank([P, P], "acc1%d%d" % (m, h), (5, 6, 1, 2)[2 * h + m])
+                acc = bank([P, P], "acc1%d%d" % (m, h), (5, 1, 2, 6)[2 * h + m])
                 multiply(acc[:], m, w_q[1], v_q1[h])
                 scale_out(y[1][m][:, h * P:(h + 1) * P], acc[:], m == 0)
         for m in range(2):

from contextlib import ExitStack

import concourse.mybir as mybir
from concourse.masks import make_identity

B, N, T, D, DV, NQ = 2, 512, 2048, 512, 256, 256
FLOPS = 2 * B * NQ * N * (D + DV)

F32 = mybir.dt.float32
BF16 = mybir.dt.bfloat16
I32 = mybir.dt.int32
U32 = mybir.dt.uint32
U16 = mybir.dt.uint16
U8 = mybir.dt.uint8
FP8X4 = mybir.dt.float8_e4m3fn_x4
ACT = mybir.ActivationFunctionType
ALU = mybir.AluOpType

P = 128
PACK = 4
ROW = P - 1
HALVES = DV // P
LIST_COLS = N // 16
TURN_STEP = 8
KB_SHARE = T * 3 // 4
VS_SHARE = T // 4
BIAS_SHARE = 256
KEYS_FIRST = T * 3 // 16


def tile_attend_sigm_kb_pgb2q256n512t2048_kernel(tc, q_words, q_scales, k_words, k_scales, vT, vs, kb, offs, out):
    nc = tc.nc
    with ExitStack() as ctx:
        sb = ctx.enter_context(tc.tile_pool(name="sb", bufs=1))
        shared = ctx.enter_context(tc.tile_pool(name="shared", bufs=1))
        ps = ctx.enter_context(tc.psum_pool(name="ps", bufs=1))

        def placed(shape, dtype, name, at):
            return shared.tile(shape, dtype, name=name, tag=name, offset=at, align_bytes=64)

        def bank(shape, name, n):
            return ps.tile(shape, F32, name=name, tag="bank%d" % n)

        vs_at = 0
        v1_at = vs_at + T * 4
        v0_at = v1_at + T * 4

        offsets = sb.tile([P, B * LIST_COLS], U16, name="offsets")
        kb_pool = sb.tile([P, T], F32, name="kb_pool")
        vs_pool = placed([P, T], F32, "vs_pool", vs_at)
        ks_pool = sb.tile([P, T], U8, name="ks_pool")
        kw_pool = sb.tile([P, T], U32, name="kw_pool")
        ident = sb.tile([P, P], F32, name="ident")
        qs = sb.tile([P, B, NQ], U8, name="qs", align_bytes=64)
        qw = sb.tile([P, B, NQ], U32, name="qw", align_bytes=64)
        warm = sb.tile([P, 2], F32, name="warm")

        def zero_on_vector(tile, rows, first, last):
            nc.vector.memset(tile[0:rows, first:last - 1], 0)
            nc.vector.memset(tile[0:rows, last - 1:last], 0)

        nc.vector.memset(qs[:].rearrange("p b q -> p (b q)").bitcast(I32), 0)
        nc.vector.memset(warm[:, 0:1], 0.0)
        nc.scalar.activation(warm[:, 1:2], warm[:, 0:1], ACT.Sigmoid)
        nc.gpsimd.memset(ks_pool[:].bitcast(I32), 0)
        zero_on_vector(kb_pool, ROW, 0, KB_SHARE)
        nc.gpsimd.memset(kb_pool[0:ROW, KB_SHARE:T], 0.0)
        zero_on_vector(vs_pool, ROW, 0, VS_SHARE)
        make_identity(nc, ident[:])
        nc.gpsimd.memset(vs_pool[0:ROW, VS_SHARE:T], 0.0)

        nc.sync.dma_start(offsets[:], offs)
        nc.sync.dma_start(kb_pool[ROW:P, :], kb[0:1, :])
        key_words = k_words[0].rearrange("p t r -> p (t r)").bitcast(I32)
        nc.sync.dma_start(kw_pool[:].bitcast(I32)[:, 0:KEYS_FIRST], key_words[:, 0:KEYS_FIRST])
        nc.sync.dma_start(vs_pool[ROW:P, :], vs[0:1, :])
        ks_rows = k_scales[0].bitcast(I32).rearrange("(a r) t -> r a t", r=4)
        for r in range(4):
            nc.sync.dma_start(ks_pool[:].bitcast(I32)[r:P:32, :], ks_rows[r])
        nc.sync.dma_start(kw_pool[:].bitcast(I32)[:, KEYS_FIRST:T], key_words[:, KEYS_FIRST:T])
        nc.sync.dma_start(qw[:].bitcast(I32), q_words.rearrange("b o p q r -> p (b o) (q r)").bitcast(I32))
        qs_rows = q_scales.bitcast(I32).rearrange("b o (a r) q -> r a (b o) q", r=4)
        for r in range(4):
            nc.sync.dma_start(qs[:].bitcast(I32)[r:P:32, :, :], qs_rows[r])
        v_pool = [placed([P, T], F32, "v_pool0", v0_at), placed([P, T], F32, "v_pool1", v1_at)]
        for h in range(HALVES):
            nc.sync.dma_start(v_pool[h][:], vT[h * P:(h + 1) * P, :])

        def entries(b, first=0, last=N):
            return offsets[:, b * LIST_COLS + first // 16:b * LIST_COLS + last // 16]

        def deal(dst, pool, b):
            nc.vector.tensor_copy(dst[:].rearrange("p t s -> p s t"), pool[:].indirect(entries(b)))

        def gather_row(pool, name, b, on_vector=0):
            row = sb.tile([P, N], F32, name="%s%d" % (name, b))
            if on_vector:
                nc.vector.tensor_copy(row[:, 0:on_vector], pool[:].indirect(entries(b, 0, on_vector)))
            nc.scalar.activation(row[:, on_vector:N], pool[:].indirect(entries(b, on_vector, N)), ACT.Copy)
            return row[:].rearrange("p (s t) -> p t s", t=PACK)

        def turn_row(dst, row, first):
            for t in reversed(range(PACK)):
                at = (first + t) * TURN_STEP
                nc.tensor.transpose(dst[:, at:at + P], row[:, t, :], ident[:])

        kb_g = [gather_row(kb_pool, "kb_g", 1, BIAS_SHARE), gather_row(kb_pool, "kb_g", 0)]
        vs_g = [gather_row(vs_pool, "vs_g", b) for b in range(B)]
        vs_d = [sb.tile([P, PACK, P], F32, name="vs_d%d" % b) for b in range(B)]
        for b in range(B):
            nc.scalar.copy(vs_d[b][:].rearrange("p t s -> p s t"), vs_g[b].rearrange("p t s -> p s t"))
        kb_bank = bank([P, N], "kb_bank", 0)
        for n, b in enumerate(reversed(range(B))):
            turn_row(kb_bank, kb_g[n], b * PACK)
        kb_col = placed([P, B * PACK], F32, "kb_col", vs_at)
        nc.scalar.copy(kb_col[:], kb_bank[:, ROW:ROW + B * PACK * TURN_STEP:TURN_STEP])

        kw_d = [sb.tile([P, PACK, P], U32, name="kw_d0", align_bytes=64), sb.tile([P, PACK, P], U32, name="kw_d1", align_bytes=64)]
        prob = [sb.tile([P, PACK, NQ], F32, name="prob%d" % b, align_bytes=64) for b in range(B)]

        def scores(b, groups):
            for n, places in groups:
                score = bank([P, len(places), NQ], "score%d%d" % (b, places[0]), n)
                for u, t in enumerate(places):
                    nc.tensor.matmul_mx(
                        out=score[:, u, :],
                        lhsT=kw_d[b][:, t, :].bitcast(FP8X4), lhsT_scale=ks_d[:, b, t, :],
                        rhs=qw[:, b, :].bitcast(FP8X4), rhs_scale=qs[:, b, :],
                        start=True, stop=True,
                    )
                for u, t in enumerate(places):
                    nc.scalar.activation(prob[b][:, t, :], score[:, u, :], ACT.Sigmoid, bias=kb_col[:, b * PACK + t:b * PACK + t + 1])

        def gather_values(v_g, h, b, on_vector):
            window = v_pool[h][:].indirect(entries(b))
            if on_vector:
                nc.vector.tensor_copy(v_g[:], window)
            else:
                nc.scalar.activation(v_g[:], window, ACT.Copy)

        def turn_values(dst, v_g):
            words = v_g[:].bitcast(F32)
            for u in range(2):
                nc.tensor.transpose(dst[:, u, :], words[:, u:N // 2:2], ident[:])

        def weave_values(v_bf, turned):
            nc.scalar.copy(v_bf[:].bitcast(F32).rearrange("p (h e u) -> p h e u", e=P, u=2), turned.rearrange("p h u e -> p h e u"))

        def quantize(values, codes, scales):
            nc.vector.quantize_mx(out=codes[:].bitcast(FP8X4), scales=scales[:], in_=values[:])
            return codes, scales

        def planes(name, width):
            return (sb.tile([P, width], U32, name=name + "_codes", align_bytes=64),
                    sb.tile([P, width], U8, name=name + "_scales", align_bytes=64))

        def weigh(b, vs_bank, w_bf):
            scale = vs_bank[:, ROW:ROW + PACK * TURN_STEP:TURN_STEP].unsqueeze(1).unsqueeze(3).to_broadcast([P, NQ // 4, PACK, 4])
            nc.vector.tensor_tensor(
                w_bf[:].rearrange("p (c i t) -> p c t i", i=4, t=PACK),
                prob[b][:].rearrange("p t (c i) -> p c t i", i=4),
                scale, ALU.mult,
            )
            return w_bf

        def multiply(acc, m, w_q, v_q):
            rows = slice(m * P, (m + 1) * P)
            nc.tensor.matmul_mx(
                out=acc,
                lhsT=w_q[0][:, rows].bitcast(FP8X4), lhsT_scale=w_q[1][:, rows],
                rhs=v_q[0][:].bitcast(FP8X4), rhs_scale=v_q[1][:],
                start=True, stop=True,
            )

        def scale_out(y, acc, on_vector):
            if on_vector:
                nc.vector.tensor_scalar(y, acc, 1.0 / 16.0, None, ALU.mult)
            else:
                nc.scalar.activation(y, acc, ACT.Copy, scale=1.0 / 16.0)

        v_g = [[sb.tile([P, N], BF16, name="v_g%d%d" % (h, b), align_bytes=64) for b in range(B)] for h in range(HALVES)]

        ks_d = sb.tile([P, B, PACK, P], U8, name="ks_d", align_bytes=64)
        nc.vector.tensor_copy(ks_d[:].rearrange("p b t s -> p b s t"), ks_pool[:].indirect(offsets[:]))
        for b in range(B):
            deal(kw_d[b], kw_pool, b)
        scores(0, [(1, (0,)), (2, (1,)), (3, (2, 3))])
        scores(1, [(4, (0, 1)), (5, (2, 3))])
        vs_bank = [bank([P, N], "vs_bank%d" % b, 1 + b) for b in range(B)]
        for b in range(B):
            turn_row(vs_bank[b], vs_d[b][:], 0)
        gather_values(v_g[0][0], 0, 0, True)
        gather_values(v_g[0][1], 0, 1, True)
        w_bf0 = weigh(0, vs_bank[0], placed([P, NQ * PACK], BF16, "w_bf0", v0_at))

        v_bank0 = bank([P, HALVES, 2, P], "v_bank0", 7)
        v_bank1 = [bank([P, 1, 2, P], "v_bank1%d" % h, (6, 0)[h]) for h in range(HALVES)]
        turn_values(v_bank0[:, 0], v_g[0][0])
        turn_values(v_bank1[0][:, 0], v_g[0][1])
        gather_values(v_g[1][0], 1, 0, False)
        turn_values(v_bank0[:, 1], v_g[1][0])
        gather_values(v_g[1][1], 1, 1, False)
        turn_values(v_bank1[1][:, 0], v_g[1][1])
        w_bf1 = weigh(1, vs_bank[1], placed([P, NQ * PACK], BF16, "w_bf1", v0_at + NQ * PACK * 2))
        w_q = [quantize(w_bf0, *planes("w0", NQ)), quantize(w_bf1, *planes("w1", NQ))]

        v_bf0 = sb.tile([P, DV * PACK], BF16, name="v_bf0", align_bytes=64)
        weave_values(v_bf0, v_bank0[:])
        v_bf1 = [placed([P, P * PACK], BF16, "v_bf10", v1_at), sb.tile([P, P * PACK], BF16, name="v_bf11", align_bytes=64)]
        for h in range(HALVES):
            weave_values(v_bf1[h], v_bank1[h][:])
        v_q0 = quantize(v_bf0, *planes("v0", DV))
        v_q1 = [quantize(v_bf1[h], *planes("v1%d" % h, P)) for h in range(HALVES)]

        y = [[sb.tile([P, DV], F32, name="y%d%d" % (b, m)) for m in range(2)] for b in range(B)]
        for m in range(2):
            acc = bank([P, DV], "acc0%d" % m, (3, 4)[m])
            multiply(acc[:], m, w_q[0], v_q0)
            scale_out(y[0][m][:], acc[:], m == 1)
            nc.sync.dma_start(out[0, m * P:(m + 1) * P, :], y[0][m][:])
        for h in range(HALVES):
            for m in range(2):
                acc = bank([P, P], "acc1%d%d" % (m, h), (5, 1, 2, 6)[2 * h + m])
                multiply(acc[:], m, w_q[1], v_q1[h])
                scale_out(y[1][m][:, h * P:(h + 1) * P], acc[:], m == 0)
        for m in range(2):
            nc.sync.dma_start(out[1, m * P:(m + 1) * P, :], y[1][m][:])
